import numpy as np, ml_dtypes
CORES = [2,3,42,43,82,83,122,123]
N = 8
import mx_ref
BF = ml_dtypes.bfloat16
def gentries(a):
    return np.ascontiguousarray(a.reshape(8, 16, -1).transpose(0, 2, 1)).reshape(8, -1)
def gtable(e):
    e = np.asarray(e); return np.ascontiguousarray(e.reshape(8, -1, 16).transpose(0, 2, 1)).reshape(128, -1).astype(np.int32)
def gcols(t, e):
    v = np.concatenate([t.reshape(8, 16, -1, 4), np.zeros((8, 16, 1, 4), BF)], axis=2)
    return np.ascontiguousarray(np.stack([v[g][:, e[g]] for g in range(8)])).reshape(128, -1)
def tile(rs):
    return np.stack(rs, axis=2).reshape(128, -1).astype(BF)
def pick(q, e):
    c = np.concatenate([q[0].reshape(128, -1, 4), np.zeros((128, 1, 4), np.uint8)], axis=1); s = np.concatenate([q[1], np.ones((16, 1), np.uint8)], axis=1)
    return (np.ascontiguousarray(c[:, e].reshape(128, -1)), np.ascontiguousarray(s[:, e]))
def join(*qs):
    return (np.concatenate([q[0] for q in qs], axis=1), np.concatenate([q[1] for q in qs], axis=1))
def put(q, e, v):
    c, s = q[0].reshape(128, -1, 4).copy(), q[1].copy(); c[:, e] = v[0].reshape(128, -1, 4); s[:, e] = v[1]
    return (c.reshape(128, -1), s)
def pk(c, s):
    return (np.ascontiguousarray(c), mx_ref.live(s))
def emit(q):
    return q[0], q[1]
def packed(v, rng):
    q = [mx_ref.quantize(np.ascontiguousarray(v[r])) for r in range(N)]
    return np.stack([a for a, b in q]), np.stack([mx_ref.plane(b, rng) for a, b in q])
def values_of_codes():
    e, c = np.zeros((128, 128, 4), np.float32), np.zeros((128, 2, 4), np.uint8)
    e[np.arange(128), np.arange(128), 0] = 1
    c[:127, :, 0] = np.arange(256).reshape(2, 128).T[:127]
    return mx_ref.matmul(mx_ref.quantize(e.reshape(128, 512).astype(BF)), (c.reshape(128, 8), np.full((16, 2), 127, np.uint8))).T.reshape(-1).astype(np.float64)
CODE_VALUE, SCALE_VALUE = values_of_codes(), 2.0 ** (np.arange(256) - 127.0)
def decode(q):
    return (CODE_VALUE[q[0]].reshape(16, 8, -1, 4) * SCALE_VALUE[q[1]][:, None, :, None] + 0.0).reshape(128, -1).astype(np.float32)
def f(rng, *shape):
    return mx_ref.flush((rng.standard_normal(shape, dtype=np.float32) * np.exp2(rng.integers(-2, 3, shape[:-1] + (1,)))).astype(BF))
def wide(rng, *shape, cols=0):
    v = rng.standard_normal(shape, dtype=np.float32) * np.exp2(rng.integers(-12, 13, shape)).astype(np.float32)
    if cols: v *= np.repeat(np.exp2(rng.integers(-cols, cols + 1, shape[:-2] + (1, shape[-1] // 4))) * (rng.random(shape[:-2] + (1, shape[-1] // 4)) > 0.0625), 4, axis=-1).astype(np.float32)
    return mx_ref.flush(v.astype(BF))
C, HALF, FAR = 384, 192, (1, 4)
def mate(r, t):
    return r ^ FAR[t]
def swap(s, t):
    lo, hi = np.arange(HALF), np.arange(HALF, C)
    return [join(pick(s[r], lo), pick(s[mate(r, t)], hi)) for r in range(N)]
def contend(e, p):
    a, b = p[:, ::2], p[:, 1::2]
    w = np.take_along_axis(e, b, axis=1) > np.take_along_axis(e, a, axis=1)
    l = np.empty_like(p)
    l[:, ::2] = np.where(w, b, a)
    l[:, 1::2] = np.where(w, a, b)
    return l
def layer(w, q):
    return [mx_ref.matmul(pick(w, np.arange(128 * b, 128 * b + 128)), q) for b in range(4)]
def clean(v):
    v = v.astype(np.float32)
    v[np.abs(v) < np.float32(2.0 ** -16)] = 0
    return v.astype(BF)
def numbers_of(rng):
    return {"x": clean(f(rng, N, 128, 4 * C)), "u": np.array(f(rng, N, 128, 512)), "v": np.array(f(rng, N, 128, 512))}
def wirings(rng):
    return {k: np.stack([gtable(np.stack([rng.permutation(C) for g in range(8)])) for r in range(N)]) for k in ("p0", "p1")}
def layers(rng, w, z):
    wc, ws = packed(np.stack([w] * N), rng)
    zc, zs = packed(np.stack([z] * N), rng)
    return {"wc": wc, "ws": ws, "zc": zc, "zs": zs}
def still(rng, k=1.0):
    w = np.zeros((128, 4, 128, 4), np.float32)
    i = np.arange(128)
    for b in range(4): w[i, b, i, b] = 32
    w = w.reshape(128, 2048)
    return layers(rng, w.astype(BF), (w * np.float32(k)).astype(BF))
def signs(rng):
    return np.stack([rng.permutation(8) % 2 * 2.0 - 1.0 for r in range(N)])
def pairs(rng, o):
    w = []
    for g in range(8):
        k = o[g].reshape(HALF, 2)[rng.permutation(HALF)]
        w.append(np.where(rng.integers(0, 2, (HALF, 1)) == 1, k[:, ::-1], k).reshape(-1))
    return np.stack(w)
def setup_inputs(rng):
    return {**numbers_of(rng), **wirings(rng), **layers(rng, np.array(f(rng, 128, 2048)), np.array(f(rng, 128, 2048)))}
def setup_inputs_ties(rng):
    d = numbers_of(rng)
    e = int(rng.integers(N))
    x = d["x"].reshape(N, 8, 16, C, 4)
    a = x[0][:, :8, :3].copy()
    a[:, :, 2] = 0
    for r in range(N):
        k = np.zeros(C, int) if r in (e, mate(e, 0)) else rng.permutation(C) % 3
        x[r][:, :8] = a[:, :, k]
    x[mate(e, 1)] = 0
    u = d["u"].reshape(N, 8, 16, 128, 4)
    for t in range(2): u[:, :, 8:, t::16] = 0
    w = np.array(f(rng, 128, 2048)).reshape(8, 16, 4, 8, 16, 4)
    w[:, 8:, :, :, :8] = 0
    return {"x": x.reshape(N, 128, 4 * C), "u": u.reshape(N, 128, 512), "v": d["v"], **wirings(rng), **layers(rng, w.reshape(128, 2048), np.array(f(rng, 128, 2048)))}
def setup_inputs_near(rng):
    d = numbers_of(rng)
    x = d["x"].astype(np.float32).reshape(N, 8, 16, C, 4)
    s = np.arange(C) // 2
    g = ((s[:, None] >> np.arange(8)) & 1) * np.exp2(np.arange(8) - 22.0)
    x[:, :, 0] = 0
    x[:, :, 0, :, 0] = 1
    x[:, :, 8] = g[:, :4]
    x[:, :, 9] = g[:, 4:]
    x[:, :, 10:] = rng.integers(4, 8, (N, 8, 6, C, 4)) * rng.choice([-1.0, 1.0], (N, 8, 6, C, 4)) * 2.0 ** -20
    one = int(rng.integers(8))
    x[:, one, 1:8] = 0
    x[:, one, 1, :, 0] = 1.75
    x[:, one, 2:4] = np.exp2(-np.arange(11.0, 19.0)).reshape(2, 1, 4)
    u = d["u"].reshape(N, 128, 128, 4)
    for t in range(2):
        u[:, :, t::16] = 0
        c = np.stack([np.exp2(-4.0 * rng.permutation(8)) for r in range(N)])
        k = (signs(rng) * c).astype(np.float32).astype(BF)
        c = c.astype(np.float32).astype(BF)
        for h in range(8):
            u[:, 16 * h, 16 * h + t, 0] = k[:, h]
            u[:, 16 * h + 8:16 * h + 10, 16 * h + t] = c[:, h][:, None, None]
    first = [pairs(rng, np.stack([np.roll(np.arange(C), -int(k)) for k in rng.permutation(8) % 2])) for r in range(N)]
    mixed = [s[contend(np.tile(s, (8, 1)), first[r])] + s for r in range(N)]
    second = []
    for r in range(N):
        k = np.concatenate([mixed[r][:, :HALF], mixed[mate(r, 1)][:, HALF:]], axis=1)
        second.append(pairs(rng, np.argsort(k, axis=1, kind="stable")))
    return {"x": x.reshape(N, 128, 4 * C).astype(BF), "u": u.reshape(N, 128, 512), "v": d["v"], "p0": np.stack([gtable(k) for k in first]), "p1": np.stack([gtable(k) for k in second]), **still(rng, 1.125)}
def setup_inputs_huge(rng):
    d = numbers_of(rng)
    x = 2.0 ** 30 * (0.6 + 0.4 * rng.random((N, 128, 4 * C)))
    u = d["u"].reshape(N, 128, 128, 4)
    for t in range(2):
        a = 2.0 ** 30 * (1 - 0.25 * rng.random((N, 128, 8, 4))) * signs(rng)[:, None, :, None]
        u[:, :, t::16] = a.astype(np.float32).astype(BF)
    return {"x": x.astype(np.float32).astype(BF), "u": u.reshape(N, 128, 512), "v": d["v"], **wirings(rng), **still(rng)}
def setup_inputs_spread(rng):
    d = setup_inputs(rng)
    d["x"] = clean(wide(rng, N, 128, 4 * C, cols=10))
    return d
def check_inputs(d):
    b = []
    for k in ("x", "u", "v"):
        a = np.abs(d[k].astype(np.float32))
        if not (np.isfinite(a).all() and ((a == 0) | (a >= 2.0 ** -30) & (a <= 2.0 ** 30)).all()): b.append("a value of " + k)
    for k in ("p0", "p1"):
        if any((np.sort(gentries(a), axis=1) != np.arange(C)).any() for a in d[k]): b.append("a group of " + k + " hasn't every number once")
    for k in ("wc", "zc"):
        if (d[k] != d[k][:1]).any(): b.append(k + " differs between ranks")
    for k in ("ws", "zs"):
        s = [mx_ref.live(p) for p in d[k]]
        if any((p != s[0]).any() for p in s): b.append(k + " differs between ranks")
    return b
def reference(x, u, v, p0, p1, wc, ws, zc, zs):
    w, z = pk(wc[0], ws[0]), pk(zc[0], zs[0])
    qu = [mx_ref.quantize(u[r]) for r in range(N)]
    now = [mx_ref.quantize(x[r]) for r in range(N)]
    kept = [[], []]
    for t in range(2):
        now = swap(now, t)
        for r in range(N):
            e = mx_ref.matmul(qu[r], now[r])[t::16] + np.float32(0.0)
            l = contend(e, gentries((p0, p1)[t][r]))
            kept[t].append(l)
            d = decode(now[r])
            p = ((gcols(d.astype(BF), l).astype(np.float32) + d) * np.float32(0.5)).astype(BF)
            now[r] = mx_ref.quantize(tile([np.maximum(a, np.float32(0.0)) * np.float32(0.03125) for a in layer(w, mx_ref.quantize(p))]))
    for t in (1, 0):
        for r in range(N):
            g = tile([a * np.float32(0.03125) for a in layer(z, now[r])])
            now[r] = mx_ref.quantize(gcols(g, np.argsort(kept[t][r], axis=1)))
        now = swap(now, t)
    y, ol = np.zeros((N, 128, C), np.float32), np.zeros((N, 8, 2 * C), np.float32)
    oc, osc = np.zeros((N, 128, 4 * C), np.uint8), np.zeros((N, 16, C), np.uint8)
    for r in range(N):
        y[r] = mx_ref.matmul(mx_ref.quantize(v[r]), now[r])
        ol[r] = np.concatenate([kept[0][r], kept[1][r]], axis=1)
        oc[r], osc[r] = emit(now[r])
    return {"y": y, "ol": ol, "oc": oc, "osc": osc}

@@ -1,0 +1,330 @@
+from concourse.mybir import dt, AluOpType, ActivationFunctionType
+
+A = AluOpType
+COPY, RELU = ActivationFunctionType.Copy, ActivationFunctionType.Relu
+C, HALF, FAR = 384, 192, (1, 4)
+SCALE = 0.03125
+ENGINES = (16, 8, 8, 16)
+F8, U8, BF, F32, I32, U16 = "float8_e4m3fn_x4", "uint8", "bfloat16", "float32", "int32", "uint16"
+
+SCRATCH = {"ps": ("psum", [128, 4096], F32)}
+
+
+def _buf(dtype, **shapes):
+    for k, n in shapes.items():
+        SCRATCH[k] = ("sbuf", [128, n], dtype)
+
+
+def _mx(**widths):
+    for k, n in widths.items():
+        SCRATCH[k] = ("sbuf", [128, n], F8)
+        SCRATCH[k + "s"] = ("sbuf", [128, n], U8)
+
+
+_buf(BF, xt=4 * C, ut=512, vt=512, eb=520)
+_buf(F32, idn=128, j8=HALF, iot=C, phf=1, sel=C, keep=C, w48=96, c48=96, cf=96, f24=96, f383=96, ff=96, yt=C)
+_buf(I32, pt=96, ipp=1, phi=1, uoi=16, fsh=96)
+_buf(U16, uof=16, pu=48)
+_mx(eq=512, uq=128, up=256, vq=128, wq=512, zq=512, fin=C)
+for _t in "01":
+    _buf(F32, **{k + _t: n for k, n in dict(sc=C, mm=C, rr=C, ll=48, lf=48, inv=C, ivw=24, lr=C).items()})
+    _buf(U16, **{k + _t: 24 for k in ("lu", "fu", "iu")})
+    _buf(BF, **{k + _t: n for k, n in dict(dd=4 * C, gt=4 * C, pm=4 * C, hh=4 * C, gg=4 * C, xx=4 * C).items()})
+    _mx(**{k + _t: n for k, n in dict(st=C, qp=C, su=HALF, bu=HALF).items()})
+_mx(sb=C, s2=C)
+
+NDMA = 24
+SEMAPHORES = ["qv", "qa", "qt", "qg"] + ["r%d" % k for k in range(4)] + ["l%d" % k for k in range(4)] + ["d%d" % k for k in range(NDMA)]
+
+
+def rank_program(g, core, T, topo):
+    me = T.rank_of(core)
+    if me is None:
+        return
+    queues = {"v": g.vector, "a": g.scalar, "t": g.tensor, "g": g, "s": g.sync}
+    count, seen, dmas = {"v": 0, "a": 0, "t": 0, "g": 0}, {}, []
+
+    def wait(q, deps):
+        need = {}
+        for s, n in deps:
+            need[s] = max(n, need.get(s, 0))
+        for s, n in need.items():
+            if seen.get((q, s), 0) < n:
+                queues[q].wait_ge(T.sem[s], n)
+                seen[(q, s)] = n
+
+    def op(q, deps, call, *args, **kw):
+        wait(q, deps)
+        call(*args, **kw).then_inc(T.sem["q" + q], 1)
+        count[q] += 1
+        return ("q" + q, count[q])
+
+    def dma(q, deps, *moves):
+        wait(q, deps)
+        s = "d%d" % len(dmas)
+        for out, in_ in moves:
+            queues[q].dma_start(out, in_).then_inc(T.sem[s], 16)
+        dmas.append((s, 16 * len(moves)))
+        return dmas[-1]
+
+    V, S, P = g.vector, g.scalar, g.tensor
+    readers, written = {b: [] for b in range(8)}, {}
+
+    def bank(b, n=HALF, at=0):
+        return T.ps[:, 512 * b + at:512 * b + at + n]
+
+    def mm(b, w, c0, x, a, n, deps):
+        assert readers[b] or b not in written
+        t = op("t", deps + readers[b], P.matmul_mx, bank(b, n), T[w][:, c0:c0 + 128], T[w + "s"][:, c0:c0 + 128],
+               T[x][:, a:a + n], T[x + "s"][:, a:a + n], True, True)
+        readers[b], written[b] = [], t
+        return t
+
+    def rd(b, t):
+        readers[b].append(t)
+        return t
+
+    def quant(q, a, tile, b, n, deps):
+        return op("v", deps, V.quantize_mx, T[q][:, a:a + n], T[q + "s"][:, a:a + n], T[tile][:, 4 * b:4 * (b + n)])
+
+    def send(k, src, land, d, deps):
+        wait("g", deps)
+        dst = T.cores[me ^ d]
+        rid, pid, _ = topo.addr(dst)
+        e = topo.engines(core, dst)[:ENGINES[k]]
+        for out, in_ in ((T[land][:, HALF:C].bitcast(dt.uint8), T[src][:, 0:HALF].bitcast(dt.uint8)),
+                         (T[land + "s"][:, HALF:C], T[src + "s"][:, 0:HALF])):
+            g.remote_dma(out_ap=out, in_ap=in_, remote_sem=T.sem["r%d" % k], local_sem=T.sem["l%d" % k],
+                         pid=pid, routing_id=rid, dma_engine_mask=sum(1 << i for i in e))
+        return ("r%d" % k, 2 * len(e)), ("l%d" % k, 2 * len(e))
+
+    def evac(q, b, out, deps, relu=False, scale=None, n=HALF):
+        src = bank(b, n)
+        if q == "v":
+            if relu:
+                return rd(b, op("v", deps, V.tensor_scalar, out, src, 0.0, SCALE, A.max, A.mult))
+            if scale:
+                return rd(b, op("v", deps, V.tensor_scalar, out, src, scale, None, A.mult))
+            return rd(b, op("v", deps, V.tensor_copy, out, src))
+        return rd(b, op("a", deps, S.activation, out, src, RELU if relu else COPY, scale=SCALE if relu else (scale or 1.0)))
+
+    d_xu = dma("s", [], (T.xt[:, 4 * HALF:4 * C], T.x[:, 4 * HALF:4 * C]))
+    d_p = dma("s", [], (T.pt[:, 0:24], T.p0[:]), (T.pt[:, 24:48], T.p1[:]),
+              (T.pt[0:128:2, 48:72], T.p0[1:128:2, :]), (T.pt[1:128:2, 48:72], T.p0[0:128:2, :]),
+              (T.pt[0:128:2, 72:96], T.p1[1:128:2, :]), (T.pt[1:128:2, 72:96], T.p1[0:128:2, :]))
+    d_xl = dma("s", [], (T.xt[:, 0:4 * HALF], T.x[:, 0:4 * HALF]))
+    d_u = dma("s", [], (T.ut[:], T.u[:]))
+
+    small = dict(allow_small_or_imprecise_dtypes=True)
+    i_id = op("g", [], g.iota, T.idn[:], [[1, 128]], 0, -1, **small)
+    i_p = op("g", [], g.iota, T.ipp[:], [[1, 1]], 0, 1)
+    i_j8 = op("g", [], g.iota, T.j8[:], [[0, 24], [1, 8]], 0, 0, **small)
+    i_uo = op("g", [], g.iota, T.uoi[:], [[1, 2], [16, 8]], 0, 0)
+    e0 = op("v", [], V.memset, T.eb[:], 0.0)
+    k0 = op("v", [], V.memset, T.keep[:], 1.0)
+    w0 = op("v", [], V.memset, T.w48[:], 0.0)
+    k0 = op("v", [k0], V.memset, T.keep[:, 0:C:16], 0.0)
+    e0 = op("v", [e0, i_id], V.tensor_scalar, T.eb[:, 3:515:4], T.idn[:], 0.0, 0.5, A.is_equal, A.mult)
+    ph = op("v", [i_p], V.tensor_scalar, T.phi[:], T.ipp[:], 15, 1, A.bitwise_and, A.logical_shift_right)
+    uo = op("v", [i_uo], V.tensor_copy, T.uof[:], T.uoi[:])
+    ph = op("v", [ph], V.tensor_copy, T.phf[:], T.phi[:])
+    for b in range(4):
+        eq = op("v", [e0], V.quantize_mx, T.eq[:, 128 * b:128 * b + 128], T.eqs[:, 128 * b:128 * b + 128], T.eb[:, 3 - b:515 - b])
+    op("v", [ph, i_j8], V.tensor_scalar, T.sel[:, 0:C:2], T.j8[:], T.phf[:], None, A.is_equal)
+    sel = op("v", [], V.tensor_scalar, T.sel[:, 1:C:2], T.j8[:], T.phf[:], -1.0, A.is_equal, A.mult)
+
+    xu = quant("su0", 0, "xt", HALF, HALF, [d_xu])
+    r0, l0 = send(0, "su0", "st0", FAR[0], [xu])
+    iot = op("g", [], g.iota, T.iot[:], [[1, C]], 0, 0, **small)
+    d_w = dma("s", [l0], (T.wq[:].bitcast(dt.uint8), T.wc[:]), (T.wqs[:], T.ws[:]))
+
+    pu = op("v", [d_p], V.tensor_copy, T.pu[:], T.pt[:, 0:48])
+    op("v", [], V.tensor_copy, T.c48[:, 1:96:2], T.pt[:, 0:48])
+    c48 = op("v", [], V.tensor_tensor, T.c48[:, 0:96:2], T.pt[:, 48:96], T.pt[:, 0:48], A.subtract)
+    fs = op("v", [], V.tensor_scalar, T.fsh[:], T.pt[:], 4, None, A.logical_shift_right)
+    op("v", [], V.tensor_scalar, T.f24[:], T.pt[:], 24.0, None, A.mult)
+    xl = quant("st0", 0, "xt", 0, HALF, [d_xl])
+
+    uq = quant("uq", 0, "ut", 0, 128, [d_u])
+    ups = op("a", [uq, uo], S.activation, T.ups[:], T.uqs[:].indirect(T.uof[:, 0:16]), COPY)
+    up = op("v", [uq, uo], V.tensor_copy, T.up[:].bitcast(dt.uint32), T.uq[:].bitcast(dt.uint32).indirect(T.uof[:, 0:16]))
+
+    fs = op("v", [fs], V.tensor_scalar, T.f383[:], T.fsh[:], -383.0, None, A.mult)
+    fs = op("v", [fs], V.tensor_tensor, T.ff[:], T.f24[:], T.f383[:], A.add)
+    op("v", [fs], V.tensor_copy, T.cf[:, 1:96:2], T.ff[:, 0:48])
+    cf = op("v", [fs], V.tensor_tensor, T.cf[:, 0:96:2], T.ff[:, 48:96], T.ff[:, 0:48], A.subtract)
+
+    def unpack(t, a, n, banks, deps):
+        return [mm(banks[b], "eq", 128 * b, "st%d" % t, a, n, deps) for b in range(4)]
+
+    def unpacked(t, a, n, banks, ms, who="aaaa"):
+        return [evac(who[b], banks[b], T["dd%d" % t][:, C * b + a:C * b + a + n], [ms[b]], n=n) for b in range(4)]
+
+    def scores(t, a, b, deps):
+        return mm(b, "up", 128 * t, "st%d" % t, a, HALF, deps)
+
+    def scored(t, a, b, m, q="v"):
+        return evac(q, b, T["sc%d" % t][:, a:a + HALF], [m])
+
+    def contend(t, a, n, deps):
+        k, e = a // 16, (a + n) // 16
+        return op("v", deps + [pu, sel], V.tensor_tensor, T["mm%d" % t][:, a:a + n],
+                  T["sc%d" % t][:, 0:C].indirect(T.pu[:, 24 * t + k:24 * t + e]), T.sel[:, a:a + n], A.mult)
+
+    def lists(t, a, n, x):
+        m, r, l, lu = T["mm%d" % t], T["rr%d" % t], T["ll%d" % t], T["lu%d" % t]
+        k, e = a // 16, (a + n) // 16
+        w = 48 * t
+        x = op("v", [x, k0], V.tensor_tensor_scan, r[:, a:a + n], T.keep[:, a:a + n], m[:, a:a + n], 0.0, A.mult, A.add)
+        x = op("v", [x, w0], V.tensor_scalar, T.w48[:, w + 2 * k + 1:w + 2 * e:2], r[:, a + 15:a + n:16], 0.0, None, A.is_lt)
+        x = op("v", [x, c48], V.tensor_tensor_scan, l[:, 2 * k:2 * e], T.w48[:, w + 2 * k:w + 2 * e],
+               T.c48[:, w + 2 * k:w + 2 * e], 0.0, A.mult, A.add)
+        return op("v", [x], V.tensor_copy, lu[:, k:e], l[:, 2 * k + 1:2 * e:2])
+
+    def places(t):
+        w = 48 * t
+        x = op("v", [cf], V.tensor_tensor_scan, T["lf%d" % t][:], T.w48[:, w:w + 48], T.cf[:, w:w + 48], 0.0, A.mult, A.add)
+        return op("v", [x], V.tensor_copy, T["fu%d" % t][:], T["lf%d" % t][:, 1:48:2])
+
+    def invert(t, deps):
+        inv = T["inv%d" % t]
+        x = op("v", deps + [iot], V.tensor_copy, inv[:, 0:C].indirect(T["fu%d" % t][:, 0:24]), T.iot[:])
+        return dma("s", [x], (T["ivw%d" % t][:], inv[0:128:16, :]))
+
+    def inverse(t, d):
+        return op("v", [d], V.tensor_copy, T["iu%d" % t][:], T["ivw%d" % t][:])
+
+    def write_lists(q, t, deps):
+        out, src = T["lr%d" % t][:], T.iot[:, 0:C].indirect(T["lu%d" % t][:, 0:24])
+        return op("v", deps + [iot], V.tensor_copy, out, src) if q == "v" else op("a", deps + [iot], S.activation, out, src, COPY)
+
+    def store_lists(t, x):
+        dma("a", [x], (T.ol[:, C * t:C * t + C], T["lr%d" % t][0:128:16, :]))
+
+    def pick_mix(t, a, rows, deps, q="a"):
+        lu, tok = T["lu%d" % t][:, a // 16:(a + HALF) // 16], []
+        for b in rows:
+            out, src = T["gt%d" % t][:, C * b + a:C * b + a + HALF], T["dd%d" % t][:, C * b:C * b + C].indirect(lu)
+            tok.append(op("v", deps, V.tensor_copy, out, src) if q == "v" else op("a", deps, S.activation, out, src, COPY))
+        return tok
+
+    def mix(t, a, banks, rows, picked, at=0):
+        for b, k in zip(rows, picked):
+            x = rd(banks[b], op("v", [k, written[banks[b]]], V.tensor_tensor, T["pm%d" % t][:, 4 * a + b:4 * (a + HALF):4],
+                                T["gt%d" % t][:, C * b + a:C * b + a + HALF], bank(banks[b], at=at), A.add))
+        return x
+
+    def layer(w, x, a, banks, deps):
+        return [mm(banks[b], w, 128 * b, x, a, HALF, deps) for b in range(4)]
+
+    def relus(t, a, banks, ms, who):
+        return [evac(who[b], banks[b], T["hh%d" % t][:, 4 * a + b:4 * (a + HALF):4], [ms[b]], relu=True) for b in range(4)]
+
+    def planes(t, a, banks, ms, who):
+        return [evac(who[b], banks[b], T["gg%d" % t][:, C * b + a:C * b + a + HALF], [ms[b]], scale=SCALE) for b in range(4)]
+
+    def undo(t, a, gl, gu, iu, who):
+        lst, tok = T["iu%d" % t][:, a // 16:(a + HALF) // 16], []
+        for b, q in enumerate(who):
+            out, src = T["xx%d" % t][:, 4 * a + b:4 * (a + HALF):4], T["gg%d" % t][:, C * b:C * b + C].indirect(lst)
+            deps = [gl[b], gu[b], iu]
+            tok.append(op("v", deps, V.tensor_copy, out, src) if q == "v" else op("a", deps, S.activation, out, src, COPY))
+        return tok
+
+    sl = scores(0, 0, 4, [xl, up, ups])
+    dl = unpack(0, 0, HALF, (0, 1, 2, 3), [xl, eq])
+    sl = scored(0, 0, 4, sl)
+    ddl = unpacked(0, 0, HALF, (0, 1, 2, 3), dl)
+
+    su = scores(0, HALF, 4, [r0, xl, up, ups])
+    su = scored(0, HALF, 4, su)
+    du = unpack(0, HALF, HALF, (5, 6, 7, 4), [r0, eq])
+    ddu = unpacked(0, HALF, HALF, (5, 6, 7, 4), du)
+    dd0 = ddl + ddu
+    lu = lists(0, HALF, HALF, contend(0, HALF, HALF, [sl, su]))
+    pa = pick_mix(0, HALF, (1, 2, 3), dd0 + [lu])
+    pv = pick_mix(0, HALF, (0,), dd0 + [lu], "v")
+    mix(0, HALF, (5, 6, 7, 4), (0,), pv)
+    cl = contend(0, 0, HALF, [sl, su])
+    x = mix(0, HALF, (5, 6, 7, 4), (1, 2, 3), pa)
+    x = quant("su1", 0, "pm0", HALF, HALF, [x])
+    r1, l1 = send(1, "su1", "qp0", FAR[1], [x])
+    d_z = dma("s", [l1], (T.zq[:].bitcast(dt.uint8), T.zc[:]), (T.zqs[:], T.zs[:]))
+    d_v = dma("s", [], (T.vt[:], T.v[:]))
+    ll = lists(0, 0, HALF, cl)
+    pa = pick_mix(0, 0, (1, 2, 3), dd0 + [ll])
+    pv = pick_mix(0, 0, (0,), dd0 + [ll], "v")
+    mix(0, 0, (0, 1, 2, 3), (0,), pv)
+    f0 = places(0)
+    x = mix(0, 0, (0, 1, 2, 3), (1, 2, 3), pa)
+    ql = quant("qp0", 0, "pm0", 0, HALF, [x])
+    ms = layer("wq", "qp0", 0, (4, 5, 6, 7), [ql, d_w])
+    hs = relus(0, 0, (4, 5, 6, 7), ms, "avav")
+    hl = quant("st1", 0, "hh0", 0, HALF, hs)
+
+    ms = layer("wq", "qp0", HALF, (0, 1, 2, 3), [r1, d_w])
+    hs = relus(0, HALF, (0, 1, 2, 3), ms, "avav")
+    sl = scores(1, 0, 4, [hl])
+    sl = scored(1, 0, 4, sl, "a")
+    hu = quant("st1", HALF, "hh0", HALF, HALF, hs)
+    su = scores(1, HALF, 0, [hu])
+    dm = unpack(1, 0, C, (5, 6, 7, 4), [hl, hu])
+    su = scored(1, HALF, 0, su)
+    dd1 = unpacked(1, 0, C, (5, 6, 7, 4), dm)
+    l1st = lists(1, 0, C, contend(1, 0, C, [sl, su]))
+    pa = pick_mix(1, 0, (0, 1, 2, 3), dd1 + [l1st])
+    pb = pick_mix(1, HALF, (0, 1, 2, 3), dd1 + [l1st])
+    d_i1 = invert(1, [places(1)])
+    x = mix(1, 0, (5, 6, 7, 4), (0, 1, 2, 3), pa)
+    qa = quant("qp1", 0, "pm1", 0, HALF, [x])
+    ma = layer("wq", "qp1", 0, (1, 2, 3, 0), [qa])
+    ha = relus(1, 0, (1, 2, 3, 0), ma, "aaaa")
+    x = mix(1, HALF, (5, 6, 7, 4), (0, 1, 2, 3), pb, HALF)
+    qb = quant("qp1", HALF, "pm1", HALF, HALF, [x])
+    mb = layer("wq", "qp1", HALF, (5, 6, 7, 4), [qb])
+    sa = quant("s2", 0, "hh1", 0, HALF, ha)
+    za = layer("zq", "s2", 0, (1, 2, 3, 0), [sa, d_z])
+    hb = relus(1, HALF, (5, 6, 7, 4), mb, "vava")
+    ga = planes(1, 0, (1, 2, 3, 0), za, "aaaa")
+    sb = quant("s2", HALF, "hh1", HALF, HALF, hb)
+    zb = layer("zq", "s2", HALF, (5, 6, 7, 4), [sb])
+    gb = planes(1, HALF, (5, 6, 7, 4), zb, "vava")
+    iu = inverse(1, d_i1)
+
+    x = undo(1, HALF, ga, gb, iu, "vava")
+    x = quant("bu1", 0, "xx1", HALF, HALF, x)
+    r2, l2 = send(2, "bu1", "sb", FAR[1], [x])
+    d_i0 = invert(0, [f0])
+    x = undo(1, 0, ga, gb, iu, "aaaa")
+    ql = quant("sb", 0, "xx1", 0, HALF, x)
+    za = layer("zq", "sb", 0, (1, 2, 3, 0), [ql])
+    ga = planes(0, 0, (1, 2, 3, 0), za, "avav")
+    vq = quant("vq", 0, "vt", 0, 128, [d_v])
+
+    zb = layer("zq", "sb", HALF, (5, 6, 7, 4), [r2])
+    gb = planes(0, HALF, (5, 6, 7, 4), zb, "avav")
+    iu = inverse(0, d_i0)
+    x = undo(0, HALF, ga, gb, iu, "avav")
+    x = quant("bu0", 0, "xx0", HALF, HALF, x)
+    r3, l3 = send(3, "bu0", "fin", FAR[0], [x])
+    x = undo(0, 0, ga, gb, iu, "avav")
+    ql = quant("fin", 0, "xx0", 0, HALF, x)
+
+    def scales(a):
+        return [(T.osc[4 * k:4 * k + 4, a:a + HALF], T.fins[32 * k:32 * k + 4, a:a + HALF]) for k in range(4)]
+
+    y = mm(5, "vq", 0, "fin", 0, HALF, [ql, vq])
+    y = evac("v", 5, T.yt[:, 0:HALF], [y])
+    dma("s", [ql], (T.oc[:, 0:4 * HALF], T.fin[:, 0:HALF].bitcast(dt.uint8)))
+    o0 = write_lists("a", 0, [lu, ll])
+    o1 = write_lists("v", 1, [l1st])
+    dma("a", [ql], *scales(0))
+    store_lists(0, o0)
+    store_lists(1, o1)
+    dma("s", [y], (T.y[:, 0:HALF], T.yt[:, 0:HALF]))
+    y = mm(6, "vq", 0, "fin", HALF, HALF, [r3])
+    y = evac("v", 6, T.yt[:, HALF:C], [y])
+    dma("s", [r3], (T.oc[:, 4 * HALF:4 * C], T.fin[:, HALF:C].bitcast(dt.uint8)))
+    dma("a", [r3], *scales(HALF))
+    dma("s", [y], (T.y[:, HALF:C], T.yt[:, HALF:C]))
+    wait("s", [("q" + q, n) for q, n in count.items()] + dmas + [r0, r1, r2, r3, l0, l1, l2, l3])

@@ -1,3 +1,4 @@
+import numpy as np
 from concourse.mybir import dt, AluOpType, ActivationFunctionType
 
 A = AluOpType
@@ -22,18 +23,20 @@ def _mx(**widths):
 
 
 _buf(BF, xt=4 * C, ut=512, vt=512, eb=520)
-_buf(F32, idn=128, j8=HALF, iot=C, phf=1, sel=C, keep=C, w48=96, c48=96, cf=96, f24=96, f383=96, ff=96, yt=C)
-_buf(I32, pt=96, ipp=1, phi=1, uoi=16, fsh=96)
-_buf(U16, uof=16, pu=48)
-_mx(eq=512, uq=128, up=256, vq=128, wq=512, zq=512, fin=C)
+_buf(F32, idn=128, j8=96, iot=C, iop=C, phf=1, sel=HALF, keep=HALF, two=96, thr=8, w48=96, c48=96, cf=48, f24=72, f383=72,
+     ff=72, yt=C, lf=48, inv=C, ivw=24, wf=C, ww=24, odd=24, even=24, flip=24, back=24)
+_buf(I32, pt=96, ipp=1, phi=1, uoi=16, fsh=72, pir=C, pia=24, pim=24, pnw=24, pno=24)
+_buf(U16, uof=16, pu=48, fu=24, f1=24, pau=24, pmu=24)
+_mx(eq=512, uq=128, up0=128, up1=128, vq=128, wq=512, zq=512, fin=C)
 for _t in "01":
-    _buf(F32, **{k + _t: n for k, n in dict(sc=C, mm=C, rr=C, ll=48, lf=48, inv=C, ivw=24, lr=C).items()})
-    _buf(U16, **{k + _t: 24 for k in ("lu", "fu", "iu")})
-    _buf(BF, **{k + _t: n for k, n in dict(dd=4 * C, gt=4 * C, pm=4 * C, hh=4 * C, gg=4 * C, xx=4 * C).items()})
+    _buf(F32, **{k + _t: n for k, n in dict(sc=C, mm=C, fl=HALF, rr=HALF, ll=48, lr=C).items()})
+    _buf(U16, **{k + _t: 24 for k in ("lu", "iu")})
+    _buf(BF, **{k + _t: n for k, n in dict(dd=4 * C, ad=4 * C, gt=4 * C, pm=4 * C, hh=4 * C, gg=4 * C, xx=4 * C).items()})
     _mx(**{k + _t: n for k, n in dict(st=C, qp=C, su=HALF, bu=HALF).items()})
+_buf(F32, rs=HALF, pnf=C, pnv=24)
 _mx(sb=C, s2=C)
 
-NDMA = 24
+NDMA = 28
 SEMAPHORES = ["qv", "qa", "qt", "qg"] + ["r%d" % k for k in range(4)] + ["l%d" % k for k in range(4)] + ["d%d" % k for k in range(NDMA)]
 
 
@@ -41,290 +44,488 @@ def rank_program(g, core, T, topo):
     me = T.rank_of(core)
     if me is None:
         return
-    queues = {"v": g.vector, "a": g.scalar, "t": g.tensor, "g": g, "s": g.sync}
-    count, seen, dmas = {"v": 0, "a": 0, "t": 0, "g": 0}, {}, []
+    V, S, P = g.vector, g.scalar, g.tensor
+    queues = {"v": V, "a": S, "t": P, "g": g, "s": g.sync}
+    count, seen, dmas, log, left = {"v": 0, "a": 0, "t": 0, "g": 0}, {}, [], {}, {}
+    clock = {}
+
+    def v(name, a=0, b=None, step=1, part=None, cast=None, by=None):
+        return (name, a, T[name].shape[1] if b is None else b, step, part, cast, by)
+
+    def bank(b, n=HALF, at=0):
+        return v("ps", 512 * b + at, 512 * b + at + n)
+
+    def ap(x):
+        if not isinstance(x, tuple):
+            return x
+        name, a, b, step, part, cast, by = x
+        r = T[name][part or slice(None), a:b:step] if step > 1 else T[name][part or slice(None), a:b]
+        r = r.bitcast(cast) if cast else r
+        return r.indirect(ap(by)) if by else r
+
+    def cells(x):
+        m = np.zeros(T[x[0]].shape[1], bool)
+        if x[0] == "ps":
+            m[x[1] // 512 * 512:x[1] // 512 * 512 + 512] = True
+        else:
+            m[x[1]:x[2]:x[3]] = True
+        return m
+
+    def hazards(q, outs, ins):
+        need = []
+        for x, writes in [(x, True) for x in outs] + [(x, False) for x in ins]:
+            m = cells(x)
+            for tok, who, wrote, k in log.get(x[0], []):
+                clash = who != q if x[0] == "ps" else wrote or (writes and who != q)
+                if clash and (m & k).any():
+                    need.append(tok)
+        return need
+
+    def note(q, tok, outs, ins):
+        for x, writes in [(x, True) for x in outs] + [(x, False) for x in ins]:
+            if x[0] in SCRATCH:
+                log.setdefault(x[0], []).append((tok, q, writes, cells(x)))
 
     def wait(q, deps):
         need = {}
         for s, n in deps:
             need[s] = max(n, need.get(s, 0))
+        know = seen.setdefault(q, {})
         for s, n in need.items():
-            if seen.get((q, s), 0) < n:
+            if know.get(s, 0) < n and not any(clock.get(x, {}).get(s, 0) >= n for x in need.items() if x[0] != s):
                 queues[q].wait_ge(T.sem[s], n)
-                seen[(q, s)] = n
+        for x in need.items():
+            for s, n in list(clock.get(x, {}).items()) + [x]:
+                know[s] = max(n, know.get(s, 0))
 
-    def op(q, deps, call, *args, **kw):
-        wait(q, deps)
-        call(*args, **kw).then_inc(T.sem["q" + q], 1)
+    def op(q, call, *args, nout=1, **kw):
+        views = [x for x in args if isinstance(x, tuple)]
+        outs, ins = views[:nout], views[nout:] + [x[6] for x in views if x[6]]
+        wait(q, hazards(q, outs, ins))
+        call(*[ap(x) for x in args], **kw).then_inc(T.sem["q" + q], 1)
         count[q] += 1
-        return ("q" + q, count[q])
+        clock[("q" + q, count[q])] = dict(seen[q])
+        note(q, ("q" + q, count[q]), outs, ins)
 
-    def dma(q, deps, *moves):
-        wait(q, deps)
+    def dma(q, *moves, after=None):
+        outs, ins = [m[0] for m in moves], [m[1] for m in moves]
+        wait(q, hazards("dma", outs, ins) + ([] if after is None else [("l%d" % after, left[after])]))
         s = "d%d" % len(dmas)
         for out, in_ in moves:
-            queues[q].dma_start(out, in_).then_inc(T.sem[s], 16)
+            queues[q].dma_start(ap(out), ap(in_)).then_inc(T.sem[s], 16)
         dmas.append((s, 16 * len(moves)))
-        return dmas[-1]
+        clock[dmas[-1]] = dict(seen[q])
+        note("dma", dmas[-1], outs, ins)
 
-    V, S, P = g.vector, g.scalar, g.tensor
-    readers, written = {b: [] for b in range(8)}, {}
-
-    def bank(b, n=HALF, at=0):
-        return T.ps[:, 512 * b + at:512 * b + at + n]
-
-    def mm(b, w, c0, x, a, n, deps):
-        assert readers[b] or b not in written
-        t = op("t", deps + readers[b], P.matmul_mx, bank(b, n), T[w][:, c0:c0 + 128], T[w + "s"][:, c0:c0 + 128],
-               T[x][:, a:a + n], T[x + "s"][:, a:a + n], True, True)
-        readers[b], written[b] = [], t
-        return t
-
-    def rd(b, t):
-        readers[b].append(t)
-        return t
-
-    def quant(q, a, tile, b, n, deps):
-        return op("v", deps, V.quantize_mx, T[q][:, a:a + n], T[q + "s"][:, a:a + n], T[tile][:, 4 * b:4 * (b + n)])
-
-    def send(k, src, land, d, deps):
-        wait("g", deps)
+    def send(k, src, land, d):
         dst = T.cores[me ^ d]
         rid, pid, _ = topo.addr(dst)
         e = topo.engines(core, dst)[:ENGINES[k]]
-        for out, in_ in ((T[land][:, HALF:C].bitcast(dt.uint8), T[src][:, 0:HALF].bitcast(dt.uint8)),
-                         (T[land + "s"][:, HALF:C], T[src + "s"][:, 0:HALF])):
-            g.remote_dma(out_ap=out, in_ap=in_, remote_sem=T.sem["r%d" % k], local_sem=T.sem["l%d" % k],
+        moves = ((v(land, HALF, C, cast=dt.uint8), v(src, cast=dt.uint8)), (v(land + "s", HALF, C), v(src + "s")))
+        wait("g", hazards("dma", [], [m[1] for m in moves]))
+        for out, in_ in moves:
+            g.remote_dma(out_ap=ap(out), in_ap=ap(in_), remote_sem=T.sem["r%d" % k], local_sem=T.sem["l%d" % k],
                          pid=pid, routing_id=rid, dma_engine_mask=sum(1 << i for i in e))
-        return ("r%d" % k, 2 * len(e)), ("l%d" % k, 2 * len(e))
+        note("far", ("r%d" % k, 2 * len(e)), [m[0] for m in moves], [])
+        left[k] = 2 * len(e)
 
-    def evac(q, b, out, deps, relu=False, scale=None, n=HALF):
-        src = bank(b, n)
+    def mm(k, w, b, x, a, n=HALF):
+        c0 = 128 * b
+        op("t", P.matmul_mx, bank(k, n), v(w, c0, c0 + 128), v(w + "s", c0, c0 + 128), v(x, a, a + n), v(x + "s", a, a + n), True, True)
+
+    def quant(q, a, tile, b, n=HALF):
+        op("v", V.quantize_mx, v(q, a, a + n), v(q + "s", a, a + n), v(tile, 4 * b, 4 * (b + n)), nout=2)
+
+    def copy(q, out, in_):
         if q == "v":
-            if relu:
-                return rd(b, op("v", deps, V.tensor_scalar, out, src, 0.0, SCALE, A.max, A.mult))
-            if scale:
-                return rd(b, op("v", deps, V.tensor_scalar, out, src, scale, None, A.mult))
-            return rd(b, op("v", deps, V.tensor_copy, out, src))
-        return rd(b, op("a", deps, S.activation, out, src, RELU if relu else COPY, scale=SCALE if relu else (scale or 1.0)))
+            op("v", V.tensor_copy, out, in_)
+        else:
+            op("a", S.activation, out, in_, COPY)
 
-    d_xu = dma("s", [], (T.xt[:, 4 * HALF:4 * C], T.x[:, 4 * HALF:4 * C]))
-    d_p = dma("s", [], (T.pt[:, 0:24], T.p0[:]), (T.pt[:, 24:48], T.p1[:]),
-              (T.pt[0:128:2, 48:72], T.p0[1:128:2, :]), (T.pt[1:128:2, 48:72], T.p0[0:128:2, :]),
-              (T.pt[0:128:2, 72:96], T.p1[1:128:2, :]), (T.pt[1:128:2, 72:96], T.p1[0:128:2, :]))
-    d_xl = dma("s", [], (T.xt[:, 0:4 * HALF], T.x[:, 0:4 * HALF]))
-    d_u = dma("s", [], (T.ut[:], T.u[:]))
+    def evac(q, out, in_, relu):
+        if q == "a":
+            op("a", S.activation, out, in_, RELU if relu else COPY, scale=SCALE)
+        elif relu:
+            op("v", V.tensor_scalar, out, in_, 0.0, SCALE, A.max, A.mult)
+        else:
+            op("v", V.tensor_scalar, out, in_, SCALE, None, A.mult)
 
-    small = dict(allow_small_or_imprecise_dtypes=True)
-    i_id = op("g", [], g.iota, T.idn[:], [[1, 128]], 0, -1, **small)
-    i_p = op("g", [], g.iota, T.ipp[:], [[1, 1]], 0, 1)
-    i_j8 = op("g", [], g.iota, T.j8[:], [[0, 24], [1, 8]], 0, 0, **small)
-    i_uo = op("g", [], g.iota, T.uoi[:], [[1, 2], [16, 8]], 0, 0)
-    e0 = op("v", [], V.memset, T.eb[:], 0.0)
-    k0 = op("v", [], V.memset, T.keep[:], 1.0)
-    w0 = op("v", [], V.memset, T.w48[:], 0.0)
-    k0 = op("v", [k0], V.memset, T.keep[:, 0:C:16], 0.0)
-    e0 = op("v", [e0, i_id], V.tensor_scalar, T.eb[:, 3:515:4], T.idn[:], 0.0, 0.5, A.is_equal, A.mult)
-    ph = op("v", [i_p], V.tensor_scalar, T.phi[:], T.ipp[:], 15, 1, A.bitwise_and, A.logical_shift_right)
-    uo = op("v", [i_uo], V.tensor_copy, T.uof[:], T.uoi[:])
-    ph = op("v", [ph], V.tensor_copy, T.phf[:], T.phi[:])
-    for b in range(4):
-        eq = op("v", [e0], V.quantize_mx, T.eq[:, 128 * b:128 * b + 128], T.eqs[:, 128 * b:128 * b + 128], T.eb[:, 3 - b:515 - b])
-    op("v", [ph, i_j8], V.tensor_scalar, T.sel[:, 0:C:2], T.j8[:], T.phf[:], None, A.is_equal)
-    sel = op("v", [], V.tensor_scalar, T.sel[:, 1:C:2], T.j8[:], T.phf[:], -1.0, A.is_equal, A.mult)
+    def fill(out, c):
+        op("v", V.memset, out, c)
 
-    xu = quant("su0", 0, "xt", HALF, HALF, [d_xu])
-    r0, l0 = send(0, "su0", "st0", FAR[0], [xu])
-    iot = op("g", [], g.iota, T.iot[:], [[1, C]], 0, 0, **small)
-    d_w = dma("s", [l0], (T.wq[:].bitcast(dt.uint8), T.wc[:]), (T.wqs[:], T.ws[:]))
+    def ts(out, in0, *rest):
+        op("v", V.tensor_scalar, out, in0, *rest)
 
-    pu = op("v", [d_p], V.tensor_copy, T.pu[:], T.pt[:, 0:48])
-    op("v", [], V.tensor_copy, T.c48[:, 1:96:2], T.pt[:, 0:48])
-    c48 = op("v", [], V.tensor_tensor, T.c48[:, 0:96:2], T.pt[:, 48:96], T.pt[:, 0:48], A.subtract)
-    fs = op("v", [], V.tensor_scalar, T.fsh[:], T.pt[:], 4, None, A.logical_shift_right)
-    op("v", [], V.tensor_scalar, T.f24[:], T.pt[:], 24.0, None, A.mult)
-    xl = quant("st0", 0, "xt", 0, HALF, [d_xl])
+    def tt(out, in0, in1, o):
+        op("v", V.tensor_tensor, out, in0, in1, o)
 
-    uq = quant("uq", 0, "ut", 0, 128, [d_u])
-    ups = op("a", [uq, uo], S.activation, T.ups[:], T.uqs[:].indirect(T.uof[:, 0:16]), COPY)
-    up = op("v", [uq, uo], V.tensor_copy, T.up[:].bitcast(dt.uint32), T.uq[:].bitcast(dt.uint32).indirect(T.uof[:, 0:16]))
+    def scan(out, d0, d1):
+        op("v", V.tensor_tensor_scan, out, d0, d1, 0.0, A.mult, A.add)
 
-    fs = op("v", [fs], V.tensor_scalar, T.f383[:], T.fsh[:], -383.0, None, A.mult)
-    fs = op("v", [fs], V.tensor_tensor, T.ff[:], T.f24[:], T.f383[:], A.add)
-    op("v", [fs], V.tensor_copy, T.cf[:, 1:96:2], T.ff[:, 0:48])
-    cf = op("v", [fs], V.tensor_tensor, T.cf[:, 0:96:2], T.ff[:, 48:96], T.ff[:, 0:48], A.subtract)
+    def iota(out, pattern, mult=0):
+        if SCRATCH[out[0]][2] == I32:
+            op("g", g.iota, out, pattern, 0, mult)
+        else:
+            op("g", g.iota, out, pattern, 0, mult, allow_small_or_imprecise_dtypes=True)
 
-    def unpack(t, a, n, banks, deps):
-        return [mm(banks[b], "eq", 128 * b, "st%d" % t, a, n, deps) for b in range(4)]
+    def plane(name, b, a, n=HALF):
+        return v(name, C * b + a, C * b + a + n)
 
-    def unpacked(t, a, n, banks, ms, who="aaaa"):
-        return [evac(who[b], banks[b], T["dd%d" % t][:, C * b + a:C * b + a + n], [ms[b]], n=n) for b in range(4)]
+    def lane(name, b, a, n=HALF):
+        return v(name, 4 * a + b, 4 * (a + n), 4)
 
-    def scores(t, a, b, deps):
-        return mm(b, "up", 128 * t, "st%d" % t, a, HALF, deps)
+    def unit(b):
+        op("v", V.quantize_mx, v("eq", 128 * b, 128 * b + 128), v("eqs", 128 * b, 128 * b + 128), v("eb", 3 - b, 515 - b), nout=2)
 
-    def scored(t, a, b, m, q="v"):
-        return evac(q, b, T["sc%d" % t][:, a:a + HALF], [m])
+    def unpack(k, t, b, a):
+        mm(k, "eq", b, "st%d" % t, a)
 
-    def contend(t, a, n, deps):
-        k, e = a // 16, (a + n) // 16
-        return op("v", deps + [pu, sel], V.tensor_tensor, T["mm%d" % t][:, a:a + n],
-                  T["sc%d" % t][:, 0:C].indirect(T.pu[:, 24 * t + k:24 * t + e]), T.sel[:, a:a + n], A.mult)
+    def unpacked(q, t, b, a, k):
+        copy(q, plane("dd%d" % t, b, a), bank(k))
 
-    def lists(t, a, n, x):
-        m, r, l, lu = T["mm%d" % t], T["rr%d" % t], T["ll%d" % t], T["lu%d" % t]
-        k, e = a // 16, (a + n) // 16
-        w = 48 * t
-        x = op("v", [x, k0], V.tensor_tensor_scan, r[:, a:a + n], T.keep[:, a:a + n], m[:, a:a + n], 0.0, A.mult, A.add)
-        x = op("v", [x, w0], V.tensor_scalar, T.w48[:, w + 2 * k + 1:w + 2 * e:2], r[:, a + 15:a + n:16], 0.0, None, A.is_lt)
-        x = op("v", [x, c48], V.tensor_tensor_scan, l[:, 2 * k:2 * e], T.w48[:, w + 2 * k:w + 2 * e],
-               T.c48[:, w + 2 * k:w + 2 * e], 0.0, A.mult, A.add)
-        return op("v", [x], V.tensor_copy, lu[:, k:e], l[:, 2 * k + 1:2 * e:2])
+    def scored(q, t, a, k):
+        copy(q, v("sc%d" % t, a, a + HALF), bank(k))
 
-    def places(t):
-        w = 48 * t
-        x = op("v", [cf], V.tensor_tensor_scan, T["lf%d" % t][:], T.w48[:, w:w + 48], T.cf[:, w:w + 48], 0.0, A.mult, A.add)
-        return op("v", [x], V.tensor_copy, T["fu%d" % t][:], T["lf%d" % t][:, 1:48:2])
+    def wired(t, a):
+        return v("sc%d" % t, by=v("pu", 24 * t + a // 16, 24 * t + (a + HALF) // 16))
 
-    def invert(t, deps):
-        inv = T["inv%d" % t]
-        x = op("v", deps + [iot], V.tensor_copy, inv[:, 0:C].indirect(T["fu%d" % t][:, 0:24]), T.iot[:])
-        return dma("s", [x], (T["ivw%d" % t][:], inv[0:128:16, :]))
+    def contend(q, t, a):
+        copy(q, v("mm%d" % t, a, a + HALF), wired(t, a))
 
-    def inverse(t, d):
-        return op("v", [d], V.tensor_copy, T["iu%d" % t][:], T["ivw%d" % t][:])
+    def flags(t, a, n=HALF):
+        tt(v("fl%d" % t, a // 2, (a + n) // 2), v("mm%d" % t, a + 1, a + n, 2), v("mm%d" % t, a, a + n, 2), A.is_gt)
 
-    def write_lists(q, t, deps):
-        out, src = T["lr%d" % t][:], T.iot[:, 0:C].indirect(T["lu%d" % t][:, 0:24])
-        return op("v", deps + [iot], V.tensor_copy, out, src) if q == "v" else op("a", deps + [iot], S.activation, out, src, COPY)
+    def digits(t, a):
+        scan(v("rr%d" % t, a // 2, a // 2 + 96), v("two"), v("fl%d" % t, a // 2, a // 2 + 96))
 
-    def store_lists(t, x):
-        dma("a", [x], (T.ol[:, C * t:C * t + C], T["lr%d" % t][0:128:16, :]))
+    def own(t, a, n=HALF):
+        ts(v("w48", 48 * t + a // 8 + 1, 48 * t + (a + n) // 8, 2), v("rr%d" % t, a // 2 + 7, (a + n) // 2, 8), v("thr", 7, 8), None, A.is_ge)
 
-    def pick_mix(t, a, rows, deps, q="a"):
-        lu, tok = T["lu%d" % t][:, a // 16:(a + HALF) // 16], []
-        for b in rows:
-            out, src = T["gt%d" % t][:, C * b + a:C * b + a + HALF], T["dd%d" % t][:, C * b:C * b + C].indirect(lu)
-            tok.append(op("v", deps, V.tensor_copy, out, src) if q == "v" else op("a", deps, S.activation, out, src, COPY))
-        return tok
+    def entries(t, a, n=HALF):
+        k, e = 48 * t + a // 8, 48 * t + (a + n) // 8
+        scan(v("ll%d" % t, a // 8, (a + n) // 8), v("w48", k, e), v("c48", k, e))
 
-    def mix(t, a, banks, rows, picked, at=0):
-        for b, k in zip(rows, picked):
-            x = rd(banks[b], op("v", [k, written[banks[b]]], V.tensor_tensor, T["pm%d" % t][:, 4 * a + b:4 * (a + HALF):4],
-                                T["gt%d" % t][:, C * b + a:C * b + a + HALF], bank(banks[b], at=at), A.add))
-        return x
+    def offsets(t, a, n=HALF):
+        copy("v", v("lu%d" % t, a // 16, (a + n) // 16), v("ll%d" % t, a // 8 + 1, (a + n) // 8, 2))
 
-    def layer(w, x, a, banks, deps):
-        return [mm(banks[b], w, 128 * b, x, a, HALF, deps) for b in range(4)]
+    def picked(t, b, a, n):
+        return v("dd%d" % t, C * b, C * b + C, by=v("lu%d" % t, a // 16, (a + n) // 16))
 
-    def relus(t, a, banks, ms, who):
-        return [evac(who[b], banks[b], T["hh%d" % t][:, 4 * a + b:4 * (a + HALF):4], [ms[b]], relu=True) for b in range(4)]
+    def mix(t, b, a, n=HALF):
+        tt(lane("pm%d" % t, b, a, n), picked(t, b, a, n), plane("ad%d" % t, b, a, n), A.add)
 
-    def planes(t, a, banks, ms, who):
-        return [evac(who[b], banks[b], T["gg%d" % t][:, C * b + a:C * b + a + HALF], [ms[b]], scale=SCALE) for b in range(4)]
+    def twin(q, t, b, a, n=HALF):
+        out, in_ = plane("ad%d" % t, b, a, n), plane("dd%d" % t, b, a, n)
+        if q == "g":
+            op("g", g.affine_select, out, in_, [[1, n]], A.is_ge, 0.0, 0, 0)
+        else:
+            copy(q, out, in_)
 
-    def undo(t, a, gl, gu, iu, who):
-        lst, tok = T["iu%d" % t][:, a // 16:(a + HALF) // 16], []
-        for b, q in enumerate(who):
-            out, src = T["xx%d" % t][:, 4 * a + b:4 * (a + HALF):4], T["gg%d" % t][:, C * b:C * b + C].indirect(lst)
-            deps = [gl[b], gu[b], iu]
-            tok.append(op("v", deps, V.tensor_copy, out, src) if q == "v" else op("a", deps, S.activation, out, src, COPY))
-        return tok
+    def pick(q, t, b, a, n=HALF):
+        copy(q, plane("gt%d" % t, b, a, n), picked(t, b, a, n))
 
-    sl = scores(0, 0, 4, [xl, up, ups])
-    dl = unpack(0, 0, HALF, (0, 1, 2, 3), [xl, eq])
-    sl = scored(0, 0, 4, sl)
-    ddl = unpacked(0, 0, HALF, (0, 1, 2, 3), dl)
+    def add(t, b, a, k, n=HALF, at=0):
+        tt(lane("pm%d" % t, b, a, n), plane("gt%d" % t, b, a, n), bank(k, n, at), A.add)
 
-    su = scores(0, HALF, 4, [r0, xl, up, ups])
-    su = scored(0, HALF, 4, su)
-    du = unpack(0, HALF, HALF, (5, 6, 7, 4), [r0, eq])
-    ddu = unpacked(0, HALF, HALF, (5, 6, 7, 4), du)
-    dd0 = ddl + ddu
-    lu = lists(0, HALF, HALF, contend(0, HALF, HALF, [sl, su]))
-    pa = pick_mix(0, HALF, (1, 2, 3), dd0 + [lu])
-    pv = pick_mix(0, HALF, (0,), dd0 + [lu], "v")
-    mix(0, HALF, (5, 6, 7, 4), (0,), pv)
-    cl = contend(0, 0, HALF, [sl, su])
-    x = mix(0, HALF, (5, 6, 7, 4), (1, 2, 3), pa)
-    x = quant("su1", 0, "pm0", HALF, HALF, [x])
-    r1, l1 = send(1, "su1", "qp0", FAR[1], [x])
-    d_z = dma("s", [l1], (T.zq[:].bitcast(dt.uint8), T.zc[:]), (T.zqs[:], T.zs[:]))
-    d_v = dma("s", [], (T.vt[:], T.v[:]))
-    ll = lists(0, 0, HALF, cl)
-    pa = pick_mix(0, 0, (1, 2, 3), dd0 + [ll])
-    pv = pick_mix(0, 0, (0,), dd0 + [ll], "v")
-    mix(0, 0, (0, 1, 2, 3), (0,), pv)
-    f0 = places(0)
-    x = mix(0, 0, (0, 1, 2, 3), (1, 2, 3), pa)
-    ql = quant("qp0", 0, "pm0", 0, HALF, [x])
-    ms = layer("wq", "qp0", 0, (4, 5, 6, 7), [ql, d_w])
-    hs = relus(0, 0, (4, 5, 6, 7), ms, "avav")
-    hl = quant("st1", 0, "hh0", 0, HALF, hs)
+    def relu(q, t, b, a, k, n=HALF):
+        evac(q, lane("hh%d" % t, b, a, n), bank(k, n), True)
 
-    ms = layer("wq", "qp0", HALF, (0, 1, 2, 3), [r1, d_w])
-    hs = relus(0, HALF, (0, 1, 2, 3), ms, "avav")
-    sl = scores(1, 0, 4, [hl])
-    sl = scored(1, 0, 4, sl, "a")
-    hu = quant("st1", HALF, "hh0", HALF, HALF, hs)
-    su = scores(1, HALF, 0, [hu])
-    dm = unpack(1, 0, C, (5, 6, 7, 4), [hl, hu])
-    su = scored(1, HALF, 0, su)
-    dd1 = unpacked(1, 0, C, (5, 6, 7, 4), dm)
-    l1st = lists(1, 0, C, contend(1, 0, C, [sl, su]))
-    pa = pick_mix(1, 0, (0, 1, 2, 3), dd1 + [l1st])
-    pb = pick_mix(1, HALF, (0, 1, 2, 3), dd1 + [l1st])
-    d_i1 = invert(1, [places(1)])
-    x = mix(1, 0, (5, 6, 7, 4), (0, 1, 2, 3), pa)
-    qa = quant("qp1", 0, "pm1", 0, HALF, [x])
-    ma = layer("wq", "qp1", 0, (1, 2, 3, 0), [qa])
-    ha = relus(1, 0, (1, 2, 3, 0), ma, "aaaa")
-    x = mix(1, HALF, (5, 6, 7, 4), (0, 1, 2, 3), pb, HALF)
-    qb = quant("qp1", HALF, "pm1", HALF, HALF, [x])
-    mb = layer("wq", "qp1", HALF, (5, 6, 7, 4), [qb])
-    sa = quant("s2", 0, "hh1", 0, HALF, ha)
-    za = layer("zq", "s2", 0, (1, 2, 3, 0), [sa, d_z])
-    hb = relus(1, HALF, (5, 6, 7, 4), mb, "vava")
-    ga = planes(1, 0, (1, 2, 3, 0), za, "aaaa")
-    sb = quant("s2", HALF, "hh1", HALF, HALF, hb)
-    zb = layer("zq", "s2", HALF, (5, 6, 7, 4), [sb])
-    gb = planes(1, HALF, (5, 6, 7, 4), zb, "vava")
-    iu = inverse(1, d_i1)
+    def scaled(q, t, b, a, k, n=HALF):
+        evac(q, plane("gg%d" % t, b, a, n), bank(k, n), False)
 
-    x = undo(1, HALF, ga, gb, iu, "vava")
-    x = quant("bu1", 0, "xx1", HALF, HALF, x)
-    r2, l2 = send(2, "bu1", "sb", FAR[1], [x])
-    d_i0 = invert(0, [f0])
-    x = undo(1, 0, ga, gb, iu, "aaaa")
-    ql = quant("sb", 0, "xx1", 0, HALF, x)
-    za = layer("zq", "sb", 0, (1, 2, 3, 0), [ql])
-    ga = planes(0, 0, (1, 2, 3, 0), za, "avav")
-    vq = quant("vq", 0, "vt", 0, 128, [d_v])
+    def undo(q, t, b, a, n=HALF):
+        copy(q, lane("xx%d" % t, b, a, n), v("gg%d" % t, C * b, C * b + C, by=v("iu%d" % t, a // 16, (a + n) // 16)))
 
-    zb = layer("zq", "sb", HALF, (5, 6, 7, 4), [r2])
-    gb = planes(0, HALF, (5, 6, 7, 4), zb, "avav")
-    iu = inverse(0, d_i0)
-    x = undo(0, HALF, ga, gb, iu, "avav")
-    x = quant("bu0", 0, "xx0", HALF, HALF, x)
-    r3, l3 = send(3, "bu0", "fin", FAR[0], [x])
-    x = undo(0, 0, ga, gb, iu, "avav")
-    ql = quant("fin", 0, "xx0", 0, HALF, x)
+    heads, ev, od = slice(0, 128, 16), slice(0, 128, 2), slice(1, 128, 2)
+    L, U, B8, W32 = 0, HALF, dt.uint8, dt.uint32
 
-    def scales(a):
-        return [(T.osc[4 * k:4 * k + 4, a:a + HALF], T.fins[32 * k:32 * k + 4, a:a + HALF]) for k in range(4)]
-
-    y = mm(5, "vq", 0, "fin", 0, HALF, [ql, vq])
-    y = evac("v", 5, T.yt[:, 0:HALF], [y])
-    dma("s", [ql], (T.oc[:, 0:4 * HALF], T.fin[:, 0:HALF].bitcast(dt.uint8)))
-    o0 = write_lists("a", 0, [lu, ll])
-    o1 = write_lists("v", 1, [l1st])
-    dma("a", [ql], *scales(0))
-    store_lists(0, o0)
-    store_lists(1, o1)
-    dma("s", [y], (T.y[:, 0:HALF], T.yt[:, 0:HALF]))
-    y = mm(6, "vq", 0, "fin", HALF, HALF, [r3])
-    y = evac("v", 6, T.yt[:, HALF:C], [y])
-    dma("s", [r3], (T.oc[:, 4 * HALF:4 * C], T.fin[:, HALF:C].bitcast(dt.uint8)))
-    dma("a", [r3], *scales(HALF))
-    dma("s", [y], (T.y[:, HALF:C], T.yt[:, HALF:C]))
-    wait("s", [("q" + q, n) for q, n in count.items()] + dmas + [r0, r1, r2, r3, l0, l1, l2, l3])
+    iota(v("idn"), [[1, 128]], -1)
+    dma("s", (v("xt", 4 * HALF, 4 * C), v("x", 4 * HALF, 4 * C)))
+    fill(v("eb"), 0.0)
+    dma("s", (v("pt", 24, 48), v("p1")))
+    fill(v("w48"), 0.0)
+    fill(v("keep"), 1.0)
+    iota(v("ipp"), [[1, 1]], 1)
+    dma("s", (v("ut"), v("u")))
+    iota(v("uoi"), [[1, 2], [16, 8]])
+    ts(v("eb", 3, 515, 4), v("idn"), 0.0, 0.5, A.is_equal, A.mult)
+    dma("s", (v("xt", 0, 4 * HALF), v("x", 0, 4 * HALF)))
+    iota(v("j8"), [[0, 12], [1, 8]])
+    ts(v("phi"), v("ipp"), 15, 1, A.bitwise_and, A.logical_shift_right)
+    unit(1)
+    dma("s", (v("pt", 0, 24), v("p0")), (v("pt", 48, 72, part=ev), v("p0", part=od)), (v("pt", 48, 72, part=od), v("p0", part=ev)))
+    unit(2)
+    iota(v("iot"), [[1, C]])
+    copy("v", v("phf"), v("phi"))
+    unit(3)
+    ts(v("two"), v("j8"), v("phf"), 2.0, A.not_equal, A.mult)
+    unit(0)
+    ts(v("sel", 1, HALF, 2), v("j8"), v("phf"), -1.0, A.is_equal, A.mult)
+    ts(v("sel", 0, HALF, 2), v("j8"), v("phf"), None, A.is_equal)
+    quant("su0", 0, "xt", U)
+    ts(v("fsh", 0, 24), v("pt", 24, 48), 4, None, A.logical_shift_right)
+    ts(v("f24", 0, 24), v("pt", 24, 48), 24.0, None, A.mult)
+    ts(v("f383", 0, 24), v("fsh", 0, 24), -383.0, None, A.mult)
+    copy("v", v("uof"), v("uoi"))
+    send(0, "su0", "st0", FAR[0])
+    tt(v("ff", 0, 24), v("f24", 0, 24), v("f383", 0, 24), A.add)
+    copy("v", v("f1"), v("ff", 0, 24))
+    quant("uq", 0, "ut", 0, 128)
+    copy("v", v("pir", by=v("f1", 0, 12)), v("iot", 0, HALF))
+    iota(v("iop"), [[HALF, 2], [1, 16], [16, 12]])
+    copy("a", v("up0s"), v("uqs", by=v("uof", 0, 8)))
+    quant("st0", L, "xt", L)
+    copy("v", v("up0", cast=W32), v("uq", cast=W32, by=v("uof", 0, 8)))
+    unpack(0, 0, 0, L)
+    scan(v("thr"), v("two", 0, 8), v("sel", 0, 16, 2))
+    fill(v("keep", 0, HALF, 16), 0.0)
+    copy("v", v("c48", 1, 48, 2), v("pt", 0, 24))
+    copy("v", v("pir", by=v("f1", 12, 24)), v("iot", HALF, C))
+    mm(4, "up0", 0, "st0", L)
+    unpacked("a", 0, 0, L, 0)
+    unpack(3, 0, 3, L)
+    unpack(1, 0, 1, L)
+    scored("a", 0, L, 4)
+    unpack(2, 0, 2, L)
+    twin("g", 0, 0, L)
+    unpacked("a", 0, 1, L, 1)
+    mm(4, "up0", 0, "st0", U)
+    copy("v", v("pu", 0, 24), v("pt", 0, 24))
+    unpacked("a", 0, 3, L, 3)
+    ts(v("fsh", 48, 72), v("pt", 48, 72), 4, None, A.logical_shift_right)
+    unpack(7, 0, 2, U)
+    tt(v("c48", 0, 48, 2), v("pt", 48, 72), v("pt", 0, 24), A.subtract)
+    ts(v("fsh", 24, 48), v("pt", 0, 24), 4, None, A.logical_shift_right)
+    unpacked("a", 0, 2, L, 2)
+    dma("s", (v("pia"), v("pir", part=heads)))
+    unpack(6, 0, 1, U)
+    scored("v", 0, U, 4)
+    unpack(5, 0, 0, U)
+    twin("g", 0, 1, L)
+    unpacked("a", 0, 2, U, 7)
+    unpack(0, 0, 3, U)
+    dma("s", (v("pt", 72, 96, part=ev), v("p1", part=od)), (v("pt", 72, 96, part=od), v("p1", part=ev)))
+    tt(v("mm0", U, C), wired(0, U), v("sel"), A.mult)
+    contend("a", 0, L)
+    dma("s", (v("wq", cast=B8), v("wc")), (v("wqs"), v("ws")), after=0)
+    unpacked("a", 0, 1, U, 6)
+    scan(v("rs"), v("keep"), v("mm0", U, C))
+    unpacked("a", 0, 0, U, 5)
+    flags(0, L)
+    twin("a", 0, 1, U)
+    ts(v("w48", 25, 48, 2), v("rs", 15, HALF, 16), 0.0, None, A.is_lt)
+    digits(0, L)
+    entries(0, U)
+    unpacked("a", 0, 3, U, 0)
+    twin("g", 0, 0, U)
+    own(0, L)
+    offsets(0, U)
+    entries(0, L)
+    mix(0, 1, U)
+    pick("a", 0, 2, U)
+    pick("a", 0, 3, U)
+    offsets(0, L)
+    mix(0, 0, U)
+    pick("a", 0, 3, L)
+    add(0, 2, U, 7)
+    pick("a", 0, 2, L)
+    add(0, 3, U, 0)
+    quant("su1", 0, "pm0", U)
+    copy("a", v("up1s"), v("uqs", by=v("uof", 8, 16)))
+    copy("v", v("pau"), v("pia"))
+    mix(0, 1, L)
+    copy("a", v("lr0"), v("iot", by=v("lu0")))
+    send(1, "su1", "qp0", FAR[1])
+    mix(0, 0, L)
+    copy("a", v("pnf"), v("iot", by=v("pau")))
+    add(0, 2, L, 2)
+    add(0, 3, L, 3)
+    ts(v("f24", 48, 72), v("pt", 48, 72), 24.0, None, A.mult)
+    quant("qp0", L, "pm0", L)
+    copy("v", v("up1", cast=W32), v("uq", cast=W32, by=v("uof", 8, 16)))
+    mm(4, "wq", 0, "qp0", L)
+    copy("v", v("pu", 24, 48), v("pt", 24, 48))
+    mm(6, "wq", 2, "qp0", L)
+    ts(v("f24", 24, 48), v("pt", 0, 24), 24.0, None, A.mult)
+    ts(v("f383", 24, 72), v("fsh", 24, 72), -383.0, None, A.mult)
+    mm(7, "wq", 3, "qp0", L)
+    tt(v("c48", 48, 96, 2), v("pt", 72, 96), v("pt", 24, 48), A.subtract)
+    relu("a", 0, 0, L, 4)
+    mm(5, "wq", 1, "qp0", L)
+    copy("v", v("c48", 49, 96, 2), v("pt", 24, 48))
+    ts(v("pim"), v("pia"), 1, None, A.logical_shift_right)
+    tt(v("ff", 24, 72), v("f24", 24, 72), v("f383", 24, 72), A.add)
+    relu("a", 0, 2, L, 6)
+    copy("v", v("pmu"), v("pim"))
+    relu("v", 0, 1, L, 5)
+    relu("a", 0, 3, L, 7)
+    mm(1, "wq", 1, "qp0", U)
+    dma("s", (v("pnv", 0, 12), v("pnf", L, HALF, part=heads)), (v("pnv", 12, 24), v("pnf", U, C, part=heads)), after=1)
+    tt(v("cf", 0, 48, 2), v("ff", 48, 72), v("ff", 24, 48), A.subtract)
+    mm(0, "wq", 0, "qp0", U)
+    copy("a", v("cf", 1, 48, 2), v("ff", 24, 48))
+    mm(3, "wq", 3, "qp0", U)
+    relu("a", 0, 1, U, 1)
+    quant("st1", L, "hh0", L)
+    mm(2, "wq", 2, "qp0", U)
+    dma("s", (v("ol", 0, C), v("lr0", part=heads)), after=1)
+    relu("a", 0, 3, U, 3)
+    relu("v", 0, 0, U, 0)
+    dma("s", (v("zq", cast=B8), v("zc")), (v("zqs"), v("zs")), after=1)
+    relu("v", 0, 2, U, 2)
+    unpack(6, 1, 2, L)
+    unpack(5, 1, 0, L)
+    quant("st1", U, "hh0", U)
+    unpack(7, 1, 3, L)
+    unpacked("a", 1, 2, L, 6)
+    mm(4, "up1", 0, "st1", L)
+    scan(v("lf"), v("w48", 0, 48), v("cf"))
+    dma("s", (v("vt"), v("v")), after=1)
+    unpacked("a", 1, 0, L, 5)
+    unpacked("v", 1, 3, L, 7)
+    mm(0, "up1", 0, "st1", U)
+    scored("a", 1, L, 4)
+    copy("v", v("fu"), v("lf", 1, 48, 2))
+    unpack(1, 1, 0, U)
+    unpack(3, 1, 3, U)
+    twin("g", 1, 0, L)
+    scored("v", 1, U, 0)
+    unpack(2, 1, 2, U)
+    unpacked("a", 1, 0, U, 1)
+    unpack(4, 1, 1, L)
+    contend("v", 1, L)
+    unpack(5, 1, 1, U)
+    contend("a", 1, U)
+    twin("g", 1, 0, U)
+    flags(1, L)
+    unpacked("a", 1, 1, L, 4)
+    digits(1, L)
+    own(1, L)
+    unpacked("a", 1, 2, U, 2)
+    flags(1, U)
+    unpacked("a", 1, 3, U, 3)
+    twin("g", 1, 1, L)
+    entries(1, L)
+    digits(1, U)
+    offsets(1, L)
+    unpacked("a", 1, 1, U, 5)
+    own(1, U)
+    mix(1, 0, L)
+    pick("a", 1, 2, L)
+    twin("g", 1, 1, U)
+    pick("a", 1, 3, L)
+    mix(1, 1, L)
+    copy("a", v("wf", L, HALF), v("fl1", by=v("pmu", 0, 12)))
+    entries(1, U)
+    add(1, 2, L, 6)
+    copy("a", v("wf", U, C), v("fl1", by=v("pmu", 12, 24)))
+    add(1, 3, L, 7)
+    offsets(1, U)
+    quant("qp1", L, "pm1", L)
+    pick("a", 1, 2, U)
+    mix(1, 0, U)
+    dma("s", (v("ww", 12, 24), v("wf", U, C, part=heads)))
+    mm(4, "wq", 2, "qp1", L)
+    dma("s", (v("ww", 0, 12), v("wf", L, HALF, part=heads)))
+    mm(1, "wq", 1, "qp1", L)
+    pick("a", 1, 3, U)
+    mm(0, "wq", 0, "qp1", L)
+    mm(5, "wq", 3, "qp1", L)
+    mix(1, 1, U)
+    relu("a", 1, 2, L, 4)
+    relu("a", 1, 0, L, 0)
+    add(1, 2, U, 2)
+    relu("a", 1, 1, L, 1)
+    add(1, 3, U, 3)
+    relu("a", 1, 3, L, 5)
+    quant("qp1", U, "pm1", U)
+    copy("v", v("pnw"), v("pnv"))
+    ts(v("pno"), v("pnw"), 1, None, A.bitwise_and)
+    tt(v("even"), v("pnw"), v("pno"), A.subtract)
+    mm(6, "wq", 0, "qp1", U)
+    copy("v", v("odd"), v("pno"))
+    quant("s2", L, "hh1", L)
+    mm(2, "wq", 2, "qp1", U)
+    mm(3, "wq", 3, "qp1", U)
+    tt(v("flip", 12, 24), v("ww", 12, 24), v("odd", 12, 24), A.not_equal)
+    relu("a", 1, 0, U, 6)
+    mm(7, "wq", 1, "qp1", U)
+    relu("v", 1, 2, U, 2)
+    mm(5, "zq", 3, "s2", L)
+    relu("a", 1, 3, U, 3)
+    mm(0, "zq", 0, "s2", L)
+    relu("v", 1, 1, U, 7)
+    mm(1, "zq", 1, "s2", L)
+    scaled("a", 1, 3, L, 5)
+    mm(4, "zq", 2, "s2", L)
+    quant("s2", U, "hh1", U)
+    scaled("a", 1, 0, L, 0)
+    tt(v("back", 12, 24), v("flip", 12, 24), v("even", 12, 24), A.add)
+    scaled("a", 1, 1, L, 1)
+    tt(v("flip", 0, 12), v("ww", 0, 12), v("odd", 0, 12), A.not_equal)
+    copy("v", v("iu1", 12, 24), v("back", 12, 24))
+    scaled("v", 1, 2, L, 4)
+    mm(2, "zq", 2, "s2", U)
+    mm(6, "zq", 0, "s2", U)
+    tt(v("back", 0, 12), v("flip", 0, 12), v("even", 0, 12), A.add)
+    mm(7, "zq", 1, "s2", U)
+    scaled("a", 1, 2, U, 2)
+    mm(3, "zq", 3, "s2", U)
+    scaled("v", 1, 0, U, 6)
+    undo("a", 1, 2, U)
+    scaled("v", 1, 1, U, 7)
+    undo("v", 1, 0, U)
+    scaled("a", 1, 3, U, 3)
+    undo("a", 1, 3, U)
+    undo("v", 1, 1, U)
+    copy("v", v("iu1", 0, 12), v("back", 0, 12))
+    quant("bu1", 0, "xx1", U)
+    undo("a", 1, 2, L)
+    copy("v", v("inv", by=v("fu")), v("iop"))
+    send(2, "bu1", "sb", FAR[1])
+    undo("a", 1, 1, L)
+    undo("a", 1, 3, L)
+    undo("a", 1, 0, L)
+    copy("a", v("lr1"), v("iot", by=v("lu1")))
+    dma("s", (v("ivw"), v("inv", part=heads)))
+    quant("sb", L, "xx1", L)
+    quant("vq", 0, "vt", 0, 128)
+    mm(1, "zq", 1, "sb", L)
+    mm(0, "zq", 0, "sb", L)
+    mm(2, "zq", 2, "sb", L)
+    scaled("v", 0, 1, L, 1)
+    mm(3, "zq", 3, "sb", L)
+    scaled("v", 0, 2, L, 2)
+    scaled("a", 0, 3, L, 3)
+    scaled("v", 0, 0, L, 0)
+    mm(5, "zq", 1, "sb", U)
+    dma("s", (v("ol", C, 2 * C), v("lr1", part=heads)), after=2)
+    mm(7, "zq", 3, "sb", U)
+    mm(4, "zq", 0, "sb", U)
+    scaled("a", 0, 1, U, 5)
+    mm(6, "zq", 2, "sb", U)
+    scaled("v", 0, 3, U, 7)
+    scaled("a", 0, 0, U, 4)
+    copy("v", v("iu0"), v("ivw"))
+    scaled("v", 0, 2, U, 6)
+    undo("a", 0, 1, U)
+    undo("v", 0, 0, U)
+    undo("a", 0, 3, U)
+    undo("v", 0, 2, U)
+    undo("a", 0, 0, L)
+    quant("bu0", 0, "xx0", U)
+    undo("a", 0, 2, L)
+    undo("v", 0, 3, L)
+    send(3, "bu0", "fin", FAR[0])
+    undo("v", 0, 1, L)
+    quant("fin", L, "xx0", L)
+    mm(0, "vq", 0, "fin", L)
+    dma("s", (v("oc", 0, 4 * HALF), v("fin", L, HALF, cast=B8)))
+    copy("v", v("yt", L, HALF), bank(0))
+    dma("s", (v("y", L, HALF), v("yt", L, HALF)))
+    mm(1, "vq", 0, "fin", U)
+    dma("s", (v("oc", 4 * HALF, 4 * C), v("fin", U, C, cast=B8)))
+    dma("a", *[(v("osc", part=slice(4 * k, 4 * k + 4)), v("fins", part=slice(32 * k, 32 * k + 4))) for k in range(4)])
+    copy("v", v("yt", U, C), bank(1))
+    dma("s", (v("y", U, C), v("yt", U, C)))
+    wait("s", [("q" + q, n) for q, n in count.items()] + dmas + [(s + str(k), n) for k, n in left.items() for s in "rl"])

import numpy as np
from concourse.mybir import dt, AluOpType, ActivationFunctionType

A = AluOpType
COPY, RELU = ActivationFunctionType.Copy, ActivationFunctionType.Relu
C, HALF, FAR = 384, 192, (1, 4)
SCALE = 0.03125
ENGINES = (16, 8, 8, 16)
F8, U8, BF, F32, I32, U16 = "float8_e4m3fn_x4", "uint8", "bfloat16", "float32", "int32", "uint16"

SCRATCH = {"ps": ("psum", [128, 4096], F32)}


def _buf(dtype, **shapes):
    for k, n in shapes.items():
        SCRATCH[k] = ("sbuf", [128, n], dtype)


def _mx(**widths):
    for k, n in widths.items():
        SCRATCH[k] = ("sbuf", [128, n], F8)
        SCRATCH[k + "s"] = ("sbuf", [128, n], U8)


_buf(BF, xt=4 * C, ut=512, vt=512, eb=520)
_buf(F32, idn=128, j8=96, iot=C, iop=C, phf=1, sel=HALF, keep=HALF, two=96, thr=8, w48=96, c48=96, cf=48, f24=72, f383=72,
     ff=72, yt=C, lf=48, inv=C, ivw=24, wf=C, ww=24, odd=24, even=24, flip=24, back=24)
_buf(I32, pt=96, ipp=1, phi=1, uoi=16, fsh=72, pir=C, pia=24, pim=24, pnw=24, pno=24)
_buf(U16, uof=16, pu=48, fu=24, f1=24, pau=24, pmu=24)
_mx(eq=512, uq=128, up0=128, up1=128, vq=128, wq=512, zq=512, fin=C)
for _t in "01":
    _buf(F32, **{k + _t: n for k, n in dict(sc=C, mm=C, fl=HALF, rr=HALF, ll=48, lr=C).items()})
    _buf(U16, **{k + _t: 24 for k in ("lu", "iu")})
    _buf(BF, **{k + _t: n for k, n in dict(dd=4 * C, ad=4 * C, gt=4 * C, pm=4 * C, hh=4 * C, gg=4 * C, xx=4 * C).items()})
    _mx(**{k + _t: n for k, n in dict(st=C, qp=C, su=HALF, bu=HALF).items()})
_buf(F32, rs=HALF, pnf=C, pnv=24)
_mx(sb=C, s2=C)

NDMA = 28
SEMAPHORES = ["qv", "qa", "qt", "qg"] + ["r%d" % k for k in range(4)] + ["l%d" % k for k in range(4)] + ["d%d" % k for k in range(NDMA)]


def rank_program(g, core, T, topo):
    me = T.rank_of(core)
    if me is None:
        return
    V, S, P = g.vector, g.scalar, g.tensor
    queues = {"v": V, "a": S, "t": P, "g": g, "s": g.sync}
    count, seen, dmas, log, left = {"v": 0, "a": 0, "t": 0, "g": 0}, {}, [], {}, {}
    clock = {}

    def v(name, a=0, b=None, step=1, part=None, cast=None, by=None):
        return (name, a, T[name].shape[1] if b is None else b, step, part, cast, by)

    def bank(b, n=HALF, at=0):
        return v("ps", 512 * b + at, 512 * b + at + n)

    def ap(x):
        if not isinstance(x, tuple):
            return x
        name, a, b, step, part, cast, by = x
        r = T[name][part or slice(None), a:b:step] if step > 1 else T[name][part or slice(None), a:b]
        r = r.bitcast(cast) if cast else r
        return r.indirect(ap(by)) if by else r

    def cells(x):
        m = np.zeros(T[x[0]].shape[1], bool)
        if x[0] == "ps":
            m[x[1] // 512 * 512:x[1] // 512 * 512 + 512] = True
        else:
            m[x[1]:x[2]:x[3]] = True
        return m

    def hazards(q, outs, ins):
        need = []
        for x, writes in [(x, True) for x in outs] + [(x, False) for x in ins]:
            m = cells(x)
            for tok, who, wrote, k in log.get(x[0], []):
                clash = who != q if x[0] == "ps" else wrote or (writes and who != q)
                if clash and (m & k).any():
                    need.append(tok)
        return need

    def note(q, tok, outs, ins):
        for x, writes in [(x, True) for x in outs] + [(x, False) for x in ins]:
            if x[0] in SCRATCH:
                log.setdefault(x[0], []).append((tok, q, writes, cells(x)))

    def wait(q, deps):
        need = {}
        for s, n in deps:
            need[s] = max(n, need.get(s, 0))
        know = seen.setdefault(q, {})
        for s, n in need.items():
            if know.get(s, 0) < n and not any(clock.get(x, {}).get(s, 0) >= n for x in need.items() if x[0] != s):
                queues[q].wait_ge(T.sem[s], n)
        for x in need.items():
            for s, n in list(clock.get(x, {}).items()) + [x]:
                know[s] = max(n, know.get(s, 0))

    def op(q, call, *args, nout=1, **kw):
        views = [x for x in args if isinstance(x, tuple)]
        outs, ins = views[:nout], views[nout:] + [x[6] for x in views if x[6]]
        wait(q, hazards(q, outs, ins))
        call(*[ap(x) for x in args], **kw).then_inc(T.sem["q" + q], 1)
        count[q] += 1
        clock[("q" + q, count[q])] = dict(seen[q])
        note(q, ("q" + q, count[q]), outs, ins)

    def dma(q, *moves, after=None):
        outs, ins = [m[0] for m in moves], [m[1] for m in moves]
        wait(q, hazards("dma", outs, ins) + ([] if after is None else [("l%d" % after, left[after])]))
        s = "d%d" % len(dmas)
        for out, in_ in moves:
            queues[q].dma_start(ap(out), ap(in_)).then_inc(T.sem[s], 16)
        dmas.append((s, 16 * len(moves)))
        clock[dmas[-1]] = dict(seen[q])
        note("dma", dmas[-1], outs, ins)

    def send(k, src, land, d):
        dst = T.cores[me ^ d]
        rid, pid, _ = topo.addr(dst)
        e = topo.engines(core, dst)[:ENGINES[k]]
        moves = ((v(land, HALF, C, cast=dt.uint8), v(src, cast=dt.uint8)), (v(land + "s", HALF, C), v(src + "s")))
        wait("g", hazards("dma", [], [m[1] for m in moves]))
        for out, in_ in moves:
            g.remote_dma(out_ap=ap(out), in_ap=ap(in_), remote_sem=T.sem["r%d" % k], local_sem=T.sem["l%d" % k],
                         pid=pid, routing_id=rid, dma_engine_mask=sum(1 << i for i in e))
        note("far", ("r%d" % k, 2 * len(e)), [m[0] for m in moves], [])
        left[k] = 2 * len(e)

    def mm(k, w, b, x, a, n=HALF):
        c0 = 128 * b
        op("t", P.matmul_mx, bank(k, n), v(w, c0, c0 + 128), v(w + "s", c0, c0 + 128), v(x, a, a + n), v(x + "s", a, a + n), True, True)

    def quant(q, a, tile, b, n=HALF):
        op("v", V.quantize_mx, v(q, a, a + n), v(q + "s", a, a + n), v(tile, 4 * b, 4 * (b + n)), nout=2)

    def copy(q, out, in_):
        if q == "v":
            op("v", V.tensor_copy, out, in_)
        else:
            op("a", S.activation, out, in_, COPY)

    def evac(q, out, in_, relu):
        if q == "a":
            op("a", S.activation, out, in_, RELU if relu else COPY, scale=SCALE)
        elif relu:
            op("v", V.tensor_scalar, out, in_, 0.0, SCALE, A.max, A.mult)
        else:
            op("v", V.tensor_scalar, out, in_, SCALE, None, A.mult)

    def fill(out, c):
        op("v", V.memset, out, c)

    def ts(out, in0, *rest):
        op("v", V.tensor_scalar, out, in0, *rest)

    def tt(out, in0, in1, o):
        op("v", V.tensor_tensor, out, in0, in1, o)

    def scan(out, d0, d1):
        op("v", V.tensor_tensor_scan, out, d0, d1, 0.0, A.mult, A.add)

    def iota(out, pattern, mult=0):
        if SCRATCH[out[0]][2] == I32:
            op("g", g.iota, out, pattern, 0, mult)
        else:
            op("g", g.iota, out, pattern, 0, mult, allow_small_or_imprecise_dtypes=True)

    def plane(name, b, a, n=HALF):
        return v(name, C * b + a, C * b + a + n)

    def lane(name, b, a, n=HALF):
        return v(name, 4 * a + b, 4 * (a + n), 4)

    def unit(b):
        op("v", V.quantize_mx, v("eq", 128 * b, 128 * b + 128), v("eqs", 128 * b, 128 * b + 128), v("eb", 3 - b, 515 - b), nout=2)

    def unpack(k, t, b, a):
        mm(k, "eq", b, "st%d" % t, a)

    def unpacked(q, t, b, a, k):
        copy(q, plane("dd%d" % t, b, a), bank(k))

    def scored(q, t, a, k):
        copy(q, v("sc%d" % t, a, a + HALF), bank(k))

    def wired(t, a):
        return v("sc%d" % t, by=v("pu", 24 * t + a // 16, 24 * t + (a + HALF) // 16))

    def contend(q, t, a):
        copy(q, v("mm%d" % t, a, a + HALF), wired(t, a))

    def flags(t, a, n=HALF):
        tt(v("fl%d" % t, a // 2, (a + n) // 2), v("mm%d" % t, a + 1, a + n, 2), v("mm%d" % t, a, a + n, 2), A.is_gt)

    def digits(t, a):
        scan(v("rr%d" % t, a // 2, a // 2 + 96), v("two"), v("fl%d" % t, a // 2, a // 2 + 96))

    def own(t, a, n=HALF):
        ts(v("w48", 48 * t + a // 8 + 1, 48 * t + (a + n) // 8, 2), v("rr%d" % t, a // 2 + 7, (a + n) // 2, 8), v("thr", 7, 8), None, A.is_ge)

    def entries(t, a, n=HALF):
        k, e = 48 * t + a // 8, 48 * t + (a + n) // 8
        scan(v("ll%d" % t, a // 8, (a + n) // 8), v("w48", k, e), v("c48", k, e))

    def offsets(t, a, n=HALF):
        copy("v", v("lu%d" % t, a // 16, (a + n) // 16), v("ll%d" % t, a // 8 + 1, (a + n) // 8, 2))

    def picked(t, b, a, n):
        return v("dd%d" % t, C * b, C * b + C, by=v("lu%d" % t, a // 16, (a + n) // 16))

    def mix(t, b, a, n=HALF):
        tt(lane("pm%d" % t, b, a, n), picked(t, b, a, n), plane("ad%d" % t, b, a, n), A.add)

    def twin(q, t, b, a, n=HALF):
        out, in_ = plane("ad%d" % t, b, a, n), plane("dd%d" % t, b, a, n)
        if q == "g":
            op("g", g.affine_select, out, in_, [[1, n]], A.is_ge, 0.0, 0, 0)
        else:
            copy(q, out, in_)

    def pick(q, t, b, a, n=HALF):
        copy(q, plane("gt%d" % t, b, a, n), picked(t, b, a, n))

    def add(t, b, a, k, n=HALF, at=0):
        tt(lane("pm%d" % t, b, a, n), plane("gt%d" % t, b, a, n), bank(k, n, at), A.add)

    def relu(q, t, b, a, k, n=HALF):
        evac(q, lane("hh%d" % t, b, a, n), bank(k, n), True)

    def scaled(q, t, b, a, k, n=HALF):
        evac(q, plane("gg%d" % t, b, a, n), bank(k, n), False)

    def undo(q, t, b, a, n=HALF):
        copy(q, lane("xx%d" % t, b, a, n), v("gg%d" % t, C * b, C * b + C, by=v("iu%d" % t, a // 16, (a + n) // 16)))

    heads, ev, od = slice(0, 128, 16), slice(0, 128, 2), slice(1, 128, 2)
    L, U, B8, W32 = 0, HALF, dt.uint8, dt.uint32

    iota(v("idn"), [[1, 128]], -1)
    dma("s", (v("xt", 4 * HALF, 4 * C), v("x", 4 * HALF, 4 * C)))
    fill(v("eb"), 0.0)
    dma("s", (v("pt", 24, 48), v("p1")))
    fill(v("w48"), 0.0)
    fill(v("keep"), 1.0)
    iota(v("ipp"), [[1, 1]], 1)
    dma("s", (v("ut"), v("u")))
    iota(v("uoi"), [[1, 2], [16, 8]])
    ts(v("eb", 3, 515, 4), v("idn"), 0.0, 0.5, A.is_equal, A.mult)
    dma("s", (v("xt", 0, 4 * HALF), v("x", 0, 4 * HALF)))
    iota(v("j8"), [[0, 12], [1, 8]])
    ts(v("phi"), v("ipp"), 15, 1, A.bitwise_and, A.logical_shift_right)
    unit(1)
    dma("s", (v("pt", 0, 24), v("p0")), (v("pt", 48, 72, part=ev), v("p0", part=od)), (v("pt", 48, 72, part=od), v("p0", part=ev)))
    unit(2)
    iota(v("iot"), [[1, C]])
    copy("v", v("phf"), v("phi"))
    unit(3)
    ts(v("two"), v("j8"), v("phf"), 2.0, A.not_equal, A.mult)
    unit(0)
    ts(v("sel", 1, HALF, 2), v("j8"), v("phf"), -1.0, A.is_equal, A.mult)
    ts(v("sel", 0, HALF, 2), v("j8"), v("phf"), None, A.is_equal)
    quant("su0", 0, "xt", U)
    ts(v("fsh", 0, 24), v("pt", 24, 48), 4, None, A.logical_shift_right)
    ts(v("f24", 0, 24), v("pt", 24, 48), 24.0, None, A.mult)
    ts(v("f383", 0, 24), v("fsh", 0, 24), -383.0, None, A.mult)
    copy("v", v("uof"), v("uoi"))
    send(0, "su0", "st0", FAR[0])
    tt(v("ff", 0, 24), v("f24", 0, 24), v("f383", 0, 24), A.add)
    copy("v", v("f1"), v("ff", 0, 24))
    quant("uq", 0, "ut", 0, 128)
    copy("v", v("pir", by=v("f1", 0, 12)), v("iot", 0, HALF))
    iota(v("iop"), [[HALF, 2], [1, 16], [16, 12]])
    copy("a", v("up0s"), v("uqs", by=v("uof", 0, 8)))
    quant("st0", L, "xt", L)
    copy("v", v("up0", cast=W32), v("uq", cast=W32, by=v("uof", 0, 8)))
    unpack(0, 0, 0, L)
    scan(v("thr"), v("two", 0, 8), v("sel", 0, 16, 2))
    fill(v("keep", 0, HALF, 16), 0.0)
    copy("v", v("c48", 1, 48, 2), v("pt", 0, 24))
    copy("v", v("pir", by=v("f1", 12, 24)), v("iot", HALF, C))
    mm(4, "up0", 0, "st0", L)
    unpacked("a", 0, 0, L, 0)
    unpack(3, 0, 3, L)
    unpack(1, 0, 1, L)
    scored("a", 0, L, 4)
    unpack(2, 0, 2, L)
    twin("g", 0, 0, L)
    unpacked("a", 0, 1, L, 1)
    mm(4, "up0", 0, "st0", U)
    copy("v", v("pu", 0, 24), v("pt", 0, 24))
    unpacked("a", 0, 3, L, 3)
    ts(v("fsh", 48, 72), v("pt", 48, 72), 4, None, A.logical_shift_right)
    unpack(7, 0, 2, U)
    tt(v("c48", 0, 48, 2), v("pt", 48, 72), v("pt", 0, 24), A.subtract)
    ts(v("fsh", 24, 48), v("pt", 0, 24), 4, None, A.logical_shift_right)
    unpacked("a", 0, 2, L, 2)
    dma("s", (v("pia"), v("pir", part=heads)))
    unpack(6, 0, 1, U)
    scored("v", 0, U, 4)
    unpack(5, 0, 0, U)
    twin("g", 0, 1, L)
    unpacked("a", 0, 2, U, 7)
    unpack(0, 0, 3, U)
    dma("s", (v("pt", 72, 96, part=ev), v("p1", part=od)), (v("pt", 72, 96, part=od), v("p1", part=ev)))
    tt(v("mm0", U, C), wired(0, U), v("sel"), A.mult)
    contend("a", 0, L)
    dma("s", (v("wq", cast=B8), v("wc")), (v("wqs"), v("ws")), after=0)
    unpacked("a", 0, 1, U, 6)
    scan(v("rs"), v("keep"), v("mm0", U, C))
    unpacked("a", 0, 0, U, 5)
    flags(0, L)
    twin("a", 0, 1, U)
    ts(v("w48", 25, 48, 2), v("rs", 15, HALF, 16), 0.0, None, A.is_lt)
    digits(0, L)
    entries(0, U)
    unpacked("a", 0, 3, U, 0)
    twin("g", 0, 0, U)
    own(0, L)
    offsets(0, U)
    entries(0, L)
    mix(0, 1, U)
    pick("a", 0, 2, U)
    pick("a", 0, 3, U)
    offsets(0, L)
    mix(0, 0, U)
    pick("a", 0, 3, L)
    add(0, 2, U, 7)
    pick("a", 0, 2, L)
    add(0, 3, U, 0)
    quant("su1", 0, "pm0", U)
    copy("a", v("up1s"), v("uqs", by=v("uof", 8, 16)))
    copy("v", v("pau"), v("pia"))
    mix(0, 1, L)
    copy("a", v("lr0"), v("iot", by=v("lu0")))
    send(1, "su1", "qp0", FAR[1])
    mix(0, 0, L)
    copy("a", v("pnf"), v("iot", by=v("pau")))
    add(0, 2, L, 2)
    add(0, 3, L, 3)
    ts(v("f24", 48, 72), v("pt", 48, 72), 24.0, None, A.mult)
    quant("qp0", L, "pm0", L)
    copy("v", v("up1", cast=W32), v("uq", cast=W32, by=v("uof", 8, 16)))
    mm(4, "wq", 0, "qp0", L)
    copy("v", v("pu", 24, 48), v("pt", 24, 48))
    mm(6, "wq", 2, "qp0", L)
    ts(v("f24", 24, 48), v("pt", 0, 24), 24.0, None, A.mult)
    ts(v("f383", 24, 72), v("fsh", 24, 72), -383.0, None, A.mult)
    mm(7, "wq", 3, "qp0", L)
    tt(v("c48", 48, 96, 2), v("pt", 72, 96), v("pt", 24, 48), A.subtract)
    relu("a", 0, 0, L, 4)
    mm(5, "wq", 1, "qp0", L)
    copy("v", v("c48", 49, 96, 2), v("pt", 24, 48))
    ts(v("pim"), v("pia"), 1, None, A.logical_shift_right)
    tt(v("ff", 24, 72), v("f24", 24, 72), v("f383", 24, 72), A.add)
    relu("a", 0, 2, L, 6)
    copy("v", v("pmu"), v("pim"))
    relu("v", 0, 1, L, 5)
    relu("a", 0, 3, L, 7)
    mm(1, "wq", 1, "qp0", U)
    dma("s", (v("pnv", 0, 12), v("pnf", L, HALF, part=heads)), (v("pnv", 12, 24), v("pnf", U, C, part=heads)), after=1)
    tt(v("cf", 0, 48, 2), v("ff", 48, 72), v("ff", 24, 48), A.subtract)
    mm(0, "wq", 0, "qp0", U)
    copy("a", v("cf", 1, 48, 2), v("ff", 24, 48))
    mm(3, "wq", 3, "qp0", U)
    relu("a", 0, 1, U, 1)
    quant("st1", L, "hh0", L)
    mm(2, "wq", 2, "qp0", U)
    dma("s", (v("ol", 0, C), v("lr0", part=heads)), after=1)
    relu("a", 0, 3, U, 3)
    relu("v", 0, 0, U, 0)
    dma("s", (v("zq", cast=B8), v("zc")), (v("zqs"), v("zs")), after=1)
    relu("v", 0, 2, U, 2)
    unpack(6, 1, 2, L)
    unpack(5, 1, 0, L)
    quant("st1", U, "hh0", U)
    unpack(7, 1, 3, L)
    unpacked("a", 1, 2, L, 6)
    mm(4, "up1", 0, "st1", L)
    scan(v("lf"), v("w48", 0, 48), v("cf"))
    dma("s", (v("vt"), v("v")), after=1)
    unpacked("a", 1, 0, L, 5)
    unpacked("v", 1, 3, L, 7)
    mm(0, "up1", 0, "st1", U)
    scored("a", 1, L, 4)
    copy("v", v("fu"), v("lf", 1, 48, 2))
    unpack(1, 1, 0, U)
    unpack(3, 1, 3, U)
    twin("g", 1, 0, L)
    scored("v", 1, U, 0)
    unpack(2, 1, 2, U)
    unpacked("a", 1, 0, U, 1)
    unpack(4, 1, 1, L)
    contend("v", 1, L)
    unpack(5, 1, 1, U)
    contend("a", 1, U)
    twin("g", 1, 0, U)
    flags(1, L)
    unpacked("a", 1, 1, L, 4)
    digits(1, L)
    own(1, L)
    unpacked("a", 1, 2, U, 2)
    flags(1, U)
    unpacked("a", 1, 3, U, 3)
    twin("g", 1, 1, L)
    entries(1, L)
    digits(1, U)
    offsets(1, L)
    unpacked("a", 1, 1, U, 5)
    own(1, U)
    mix(1, 0, L)
    pick("a", 1, 2, L)
    twin("g", 1, 1, U)
    pick("a", 1, 3, L)
    mix(1, 1, L)
    copy("a", v("wf", L, HALF), v("fl1", by=v("pmu", 0, 12)))
    entries(1, U)
    add(1, 2, L, 6)
    copy("a", v("wf", U, C), v("fl1", by=v("pmu", 12, 24)))
    add(1, 3, L, 7)
    offsets(1, U)
    quant("qp1", L, "pm1", L)
    pick("a", 1, 2, U)
    mix(1, 0, U)
    dma("s", (v("ww", 12, 24), v("wf", U, C, part=heads)))
    mm(4, "wq", 2, "qp1", L)
    dma("s", (v("ww", 0, 12), v("wf", L, HALF, part=heads)))
    mm(1, "wq", 1, "qp1", L)
    pick("a", 1, 3, U)
    mm(0, "wq", 0, "qp1", L)
    mm(5, "wq", 3, "qp1", L)
    mix(1, 1, U)
    relu("a", 1, 2, L, 4)
    relu("a", 1, 0, L, 0)
    add(1, 2, U, 2)
    relu("a", 1, 1, L, 1)
    add(1, 3, U, 3)
    relu("a", 1, 3, L, 5)
    quant("qp1", U, "pm1", U)
    copy("v", v("pnw"), v("pnv"))
    ts(v("pno"), v("pnw"), 1, None, A.bitwise_and)
    tt(v("even"), v("pnw"), v("pno"), A.subtract)
    mm(6, "wq", 0, "qp1", U)
    copy("v", v("odd"), v("pno"))
    quant("s2", L, "hh1", L)
    mm(2, "wq", 2, "qp1", U)
    mm(3, "wq", 3, "qp1", U)
    tt(v("flip", 12, 24), v("ww", 12, 24), v("odd", 12, 24), A.not_equal)
    relu("a", 1, 0, U, 6)
    mm(7, "wq", 1, "qp1", U)
    relu("v", 1, 2, U, 2)
    mm(5, "zq", 3, "s2", L)
    relu("a", 1, 3, U, 3)
    mm(0, "zq", 0, "s2", L)
    relu("v", 1, 1, U, 7)
    mm(1, "zq", 1, "s2", L)
    scaled("a", 1, 3, L, 5)
    mm(4, "zq", 2, "s2", L)
    quant("s2", U, "hh1", U)
    scaled("a", 1, 0, L, 0)
    tt(v("back", 12, 24), v("flip", 12, 24), v("even", 12, 24), A.add)
    scaled("a", 1, 1, L, 1)
    tt(v("flip", 0, 12), v("ww", 0, 12), v("odd", 0, 12), A.not_equal)
    copy("v", v("iu1", 12, 24), v("back", 12, 24))
    scaled("v", 1, 2, L, 4)
    mm(2, "zq", 2, "s2", U)
    mm(6, "zq", 0, "s2", U)
    tt(v("back", 0, 12), v("flip", 0, 12), v("even", 0, 12), A.add)
    mm(7, "zq", 1, "s2", U)
    scaled("a", 1, 2, U, 2)
    mm(3, "zq", 3, "s2", U)
    scaled("v", 1, 0, U, 6)
    undo("a", 1, 2, U)
    scaled("v", 1, 1, U, 7)
    undo("v", 1, 0, U)
    scaled("a", 1, 3, U, 3)
    undo("a", 1, 3, U)
    undo("v", 1, 1, U)
    copy("v", v("iu1", 0, 12), v("back", 0, 12))
    quant("bu1", 0, "xx1", U)
    undo("a", 1, 2, L)
    copy("v", v("inv", by=v("fu")), v("iop"))
    send(2, "bu1", "sb", FAR[1])
    undo("a", 1, 1, L)
    undo("a", 1, 3, L)
    undo("a", 1, 0, L)
    copy("a", v("lr1"), v("iot", by=v("lu1")))
    dma("s", (v("ivw"), v("inv", part=heads)))
    quant("sb", L, "xx1", L)
    quant("vq", 0, "vt", 0, 128)
    mm(1, "zq", 1, "sb", L)
    mm(0, "zq", 0, "sb", L)
    mm(2, "zq", 2, "sb", L)
    scaled("v", 0, 1, L, 1)
    mm(3, "zq", 3, "sb", L)
    scaled("v", 0, 2, L, 2)
    scaled("a", 0, 3, L, 3)
    scaled("v", 0, 0, L, 0)
    mm(5, "zq", 1, "sb", U)
    dma("s", (v("ol", C, 2 * C), v("lr1", part=heads)), after=2)
    mm(7, "zq", 3, "sb", U)
    mm(4, "zq", 0, "sb", U)
    scaled("a", 0, 1, U, 5)
    mm(6, "zq", 2, "sb", U)
    scaled("v", 0, 3, U, 7)
    scaled("a", 0, 0, U, 4)
    copy("v", v("iu0"), v("ivw"))
    scaled("v", 0, 2, U, 6)
    undo("a", 0, 1, U)
    undo("v", 0, 0, U)
    undo("a", 0, 3, U)
    undo("v", 0, 2, U)
    undo("a", 0, 0, L)
    quant("bu0", 0, "xx0", U)
    undo("a", 0, 2, L)
    undo("v", 0, 3, L)
    send(3, "bu0", "fin", FAR[0])
    undo("v", 0, 1, L)
    quant("fin", L, "xx0", L)
    mm(0, "vq", 0, "fin", L)
    dma("s", (v("oc", 0, 4 * HALF), v("fin", L, HALF, cast=B8)))
    copy("v", v("yt", L, HALF), bank(0))
    dma("s", (v("y", L, HALF), v("yt", L, HALF)))
    mm(1, "vq", 0, "fin", U)
    dma("s", (v("oc", 4 * HALF, 4 * C), v("fin", U, C, cast=B8)))
    dma("a", *[(v("osc", part=slice(4 * k, 4 * k + 4)), v("fins", part=slice(32 * k, 32 * k + 4))) for k in range(4)])
    copy("v", v("yt", U, C), bank(1))
    dma("s", (v("y", U, C), v("yt", U, C)))
    wait("s", [("q" + q, n) for q, n in count.items()] + dmas + [(s + str(k), n) for k, n in left.items() for s in "rl"])
